import numpy as np, ml_dtypes
CORES = [13,21,141,149]
N = 4
BF = ml_dtypes.bfloat16
Q, W, ND, T, S, SH, KS, WM, DM = 256, 2048, 1024, 5, 1, 5, 29, 8, 4
def pick(a, i):
    return np.take_along_axis(a, i.reshape(N, 8, 1, -1), 3).reshape((N, 8, 16) + i.shape[2:])
def bf(a):
    return np.ascontiguousarray(a).astype(np.float32).astype(BF)
def limits(rng, X, lo, hi):
    s = np.sort(np.add.reduce(np.abs(pick(X, rng.integers(0, W, (N, 8, 512))) - pick(X, rng.integers(0, W, (N, 8, 512)))), axis=2), axis=2)
    return np.concatenate([np.take_along_axis(s, rng.choice(np.array(v), (N, 8, 1)), 2) for v in (lo, hi)], axis=2)
def parts(rng):
    top = rng.choice(np.array([64, 128, 256]), (1, 8, 1, 1)) - 1
    X = rng.integers(0, 256, (N, 8, 16, W)) & top; z = rng.integers(0, 256, (N, 8, 16, Q)) & top
    DL = rng.integers(0, 256, (N, 8, 16, ND)); L = rng.integers(0, 256, (N, 8, 16, Q)); R = rng.integers(0, 256, (N, 8, 16, Q))
    n = rng.integers(1, 5, (N, 8, Q)); kp = rng.integers(0, 256, (N, 8, 16, 1)); w = rng.integers(0, 256, (N, 8, 16, 1))
    return X, DL, L, R, z, n, kp, w, limits(rng, X, [10, 26, 51, 77], [410, 450, 480])
def pack(X, DL, L, R, z, n, kp, w, lm):
    return {"stock": bf(X.reshape(N, 128, W)), "donor": bf(DL.reshape(N, 128, ND)), "lend": bf(L.reshape(N, 128, Q)), "rend": bf(R.reshape(N, 128, Q)), "zed": bf(z.reshape(N, 128, Q)),
            "cnt": n.astype(np.int32), "kap": kp.reshape(N, 128, 1).astype(np.int32), "wt": w.reshape(N, 128, 1).astype(np.int32), "lim": lm.astype(np.int32)}
def setup_inputs(rng):
    return pack(*parts(rng))
def setup_inputs_spread(rng):
    def col(m): return (np.exp2(8 * rng.random((N, 8, 1, m))) * rng.random((N, 8, 16, m))).astype(np.int64)
    def few(m): return np.exp2(8 * rng.random((N, 8, 16, m))).astype(np.int64) - rng.integers(0, 2, (N, 8, 16, m))
    X, z = col(W), col(Q)
    return pack(X, few(ND), few(Q), few(Q), z, rng.choice(np.array([1, 1, 1, 2, 3, 4]), (N, 8, Q)), few(1), few(1), limits(rng, X, [1, 10, 40, 120, 300], [200, 400, 460, 490, 508]))
def ends(rng, m):
    k = rng.integers(0, 3, (N, 8, 1, m))
    return np.where(k == 2, 255 * rng.integers(0, 2, (N, 8, 16, m)), 255 * k)
def setup_inputs_ends(rng):
    X, DL, L, R, z = ends(rng, W), ends(rng, ND), ends(rng, Q), ends(rng, Q), ends(rng, Q)
    n = 1 + 3 * rng.integers(0, 2, (N, 8, Q)); kp = 255 * rng.integers(0, 2, (N, 8, 16, 1)); w = 255 * rng.integers(0, 2, (N, 8, 16, 1))
    kp[:, :, 3] = 0; kp[:, :, 15] = 255; w[:, :, 2] = 0; w[:, :, 5] = 255; w[:, 4] = 255
    n[:, :, 0] = 4; n[:, :, 1] = 1; n[:, :, Q - 2] = 1; n[:, :, Q - 1] = 4
    for g in (0, 6):
        w[:, g, 14] = 1; w[:, g, 15] = 16
        for i in (0, 3, Q - 1): z[:, g, :, i] = 0; z[:, g, 14, i] = 15; z[:, g, 15, i] = 255
    for i in (2, 5, Q - 1): z[:, 7, :, i] = 0; z[:, 5, :, i] = 0
    X[:, 7, :, 0] = 255; X[:, 5, :, 0] = 0
    for i in (1, 4, Q - 1): z[:, 4, :, i] = 255
    lm = 4080 * rng.integers(0, 2, (N, 8, 2))
    lm[:, 2, 0] = 0; lm[:, 3, 0] = 4080; lm[:, 0, 1] = 0; lm[:, 1, 1] = 4080; lm[:, 7, 1] = 4080; lm[N - 1, :, 0] = 4080
    return pack(X, DL, L, R, z, n, kp, w, lm)
def far(d):
    return np.minimum(np.maximum(d - 255 * np.arange(16), 0), 255)
def setup_inputs_corners(rng):
    X, DL, L, R, z, n, kp, w, lm = parts(rng); o = KS * np.arange(16); k = np.arange(16)[:, None]
    for q in range(N):
        for g in range(8):
            j = (g // 2 + q) % 4
            if g % 2 == 1 and j == 3: continue
            w[q, g] = 0; DL[q, g, :, 0] = 0
            if g % 2 == 0:
                b = (2, 5, 15, 16)[j]; s = int(rng.integers(20, 100)); v = int(rng.integers(20, 100))
                y = np.full((16, 16), 100); y[0, b:] += s
            else:
                b = 7; s, v = ((4080, 4079), (2049, 2048), (1, 0))[j]
                y = np.zeros((16, 16), np.int64); y[:, b:] = far(s)[:, None]
            for e in range(3):
                X[q, g][:, o + e] = y + far((0, v, v + 1)[e])[:, None] * np.where(y >= 128, -1, 1)
            sb = s if q == 1 else s - 1
            lm[q, g, 0] = v; lm[q, g, 1] = sb
            m = n[q, g]; f = np.where((b > m) & (sb < s), b, 16)
            c = rng.integers(0, 6, Q); p = np.choose(c, [m - 1, m, f - 1, f, 15 + 0 * m, 16 + 0 * m])
            late = np.where((c == 0) | (c == 3), 2, rng.integers(1, 3, (16, Q)))
            R[q, g] = np.where(k == p, 1, np.where(k < p, 2, late))
    return pack(X, DL, L, R, z, n, kp, w, lm)
def setup_inputs_crowd(rng):
    X, DL, L, R, z, n, kp, w, lm = parts(rng); o = KS * np.arange(16)
    lm[:, :, 0] = 4080; lm[4:, :, 0] = rng.choice(np.array([0, 4080]), (N - 4, 8))
    s = (3 - S) % N
    for v in (DL, L, R): v[s] = np.minimum(v[s], 253)
    def plant(q, g, who):
        w[q, g] = 0; DL[q, g, :, 0] = 0; X[q, g][:, o] = 0; X[q, g][:, o + 1] = 255
        R[q, g] = np.where(who, 0, 1); lm[q, g, 0] = rng.choice(np.array([0, 4079])); lm[q, g, 1] = rng.choice(np.array([0, 4080]))
    i = np.arange(Q)
    plant(0, 7, i >= 0); plant(1, 0, i < Q - 1)
    for g in range(8):
        plant(2, g, i < 0); plant(3, g, (i == 0) & (g == 7))
    DL[3, :, :, 1] = 255 - (np.arange(16) & 1); lm[3, :, 0] = 0; lm[3, ::2, 1] = 0
    return pack(X, DL, L, R, z, n, kp, w, lm)
def setup_inputs_ties(rng):
    X, DL, L, R, z, n, kp, w, lm = parts(rng)
    pal = np.repeat(rng.integers(0, 256, (1, 8, 16, 5)), N, axis=0)
    X = pick(pal, rng.integers(0, 5, (N, 8, W))); z = pick(pal, rng.integers(0, 5, (N, 8, Q)))
    kp = rng.choice(np.array([0, 1, 7, 128, 255]), kp.shape); few = np.array([0, 1, 3, 100, 254, 255])
    DL[:, ::2] = rng.choice(few, (N, 4, 16, ND)); R[:, 1::2] = rng.choice(few, (N, 4, 16, Q))
    return pack(X, DL, L, R, z, n, kp, w, limits(rng, X, [10, 51, 150, 256], [150, 256, 400, 480]))
def check_inputs(d):
    bad = []
    for k, lo, hi in (("stock", 0, 255), ("donor", 0, 255), ("lend", 0, 255), ("rend", 0, 255), ("zed", 0, 255), ("cnt", 1, 4), ("kap", 0, 255), ("wt", 0, 255), ("lim", 0, 4080)):
        v = np.asarray(d[k]).astype(np.float64)
        if not np.all((v >= lo) & (v <= hi)): bad.append("range of " + k)
        elif not np.all(v == np.floor(v)): bad.append("whole numbers of " + k)
    return bad
def reference(stock, donor, lend, rend, zed, cnt, kap, wt, lim):
    def whole(a, m): return np.asarray(a).astype(np.float32).astype(np.int64).reshape(N, 8, 16, m)
    X, DL, L, R, z = whole(stock, W), whole(donor, ND), whole(lend, Q), whole(rend, Q), whole(zed, Q)
    n = cnt.astype(np.int64); kp, w = whole(kap, 1), whole(wt, 1)
    th = lim[:, :, 0].astype(np.int64)[:, :, None, None]; sb = lim[:, :, 1].astype(np.int64)[:, :, None, None]
    k = np.arange(16)[:, None]; lane = np.arange(Q); A = np.zeros((N, 1, 1, 1), np.int64)
    for t in range(T):
        if t > 0: L, R, z, n = [np.roll(v, S, axis=0) for v in (L, R, z, n)]
        u = np.add.reduce(w * z, axis=2) & 4095
        ub = u[:, :, None]; nb = n[:, :, None]
        c = ((ub * ub >> SH) + kp * ub + A) & (W - 1)
        m = np.argmin(np.add.reduce(np.abs(pick(X, c) - z[:, :, :, None]), axis=2), axis=2)
        c = np.take_along_axis(c, m[:, :, None], 2)[:, :, 0]
        xc = pick(X, c); D = pick(DL, c & (ND - 1))
        y = pick(X, ((D * ub >> SH) + D + KS * k) & (W - 1))
        h = pick(X, ((R * ub >> SH) + R + KS * k) & (W - 1))
        jump = np.add.reduce(np.abs(y[:, :, :, 1:] - y[:, :, :, :-1]), axis=2)
        f = np.min(np.where((jump > sb) & (k[1:] > nb), k[1:], 16), axis=2); fb = f[:, :, None]
        meet = (np.add.reduce(np.abs(y - h), axis=2) <= th) & (k >= nb) & (k < fb)
        a = np.min(np.where(meet, k, 16), axis=2); ab = a[:, :, None]
        found = a < 16; e = np.where(found, a, f - 1)
        ye = np.take_along_axis(y, e[:, :, None, None], 3)[:, :, :, 0]
        L = np.where((k >= nb) & (k < fb), D, L); L = np.where(k >= ab, R, L)
        done = found | (f == 16)
        R = np.where(done[:, :, None], L, R); n = np.where(done, 1 + (u & 3), f)
        z = (z + ye) >> 1
        ix = np.broadcast_to((WM * lane + (u & (WM - 1)))[:, :, None], (N, 8, 16, Q)); np.put_along_axis(X, ix, (xc + ye) >> 1, 3)
        ix = np.broadcast_to((DM * lane + (u & (DM - 1)))[:, :, None], (N, 8, 16, Q))
        np.put_along_axis(DL, ix, np.where(done[:, :, None], L, np.take_along_axis(DL, ix, 3)), 3)
        A = np.add.reduce(found.astype(np.int64).reshape(N, -1), axis=1).reshape(N, 1, 1, 1)
    return {"yl": bf(L.reshape(N, 128, Q)), "yr": bf(R.reshape(N, 128, Q)), "yd": bf(DL.reshape(N, 128, ND)), "yx": bf(X.reshape(N, 128, W)), "yz": bf(z.reshape(N, 128, Q)), "yn": n.astype(np.float32)}

@@ -1,0 +1,633 @@
+from concourse.mybir import AluOpType, ActivationFunctionType
+
+OP = AluOpType
+AF = ActivationFunctionType
+LANES, HALF, NQ, VISITS = 256, 128, 8, 5
+W, EXT, ND = 2048, 448, 1024
+MAGIC = 25165824.0
+
+GS, HS, YE = (128, 0), (128, 64), ("ss", "sv")
+
+SCRATCH = {
+    "pi": ("sbuf", [128, 8448], "int32"), "pf": ("sbuf", [128, 3072], "float32"),
+    "pb": ("sbuf", [128, 52000], "bfloat16"), "pu": ("sbuf", [128, 2048], "uint16"),
+    "xs": ("sbuf", [128, W + EXT], "bfloat16"), "dn": ("sbuf", [128, 2 * ND], "bfloat16"),
+    "zed0": ("sbuf", [128, LANES], "bfloat16"), "rend0": ("sbuf", [128, LANES], "bfloat16"),
+    "lend0": ("sbuf", [128, LANES], "bfloat16"), "cnt0": ("sbuf", [8, LANES], "int32"),
+    "kap0": ("sbuf", [128, 1], "int32"), "wt0": ("sbuf", [128, 1], "int32"), "lim0": ("sbuf", [8, 2], "int32"),
+    "yn0": ("sbuf", [8, LANES], "float32"), "yz0": ("sbuf", [128, LANES], "bfloat16"),
+}
+SEMAPHORES = ["sv", "ss", "st", "sg", "zsent", "rsent"]
+for _i in range(8):
+    SCRATCH["ps%d" % _i] = ("psum", [128, 512], "float32")
+for _i in range(24):
+    SEMAPHORES.append("dma%d" % _i)
+for _t in range(VISITS):
+    for _b in range(2):
+        SCRATCH["zo%d%d" % (_t, _b)] = ("sbuf", [128, HALF], "bfloat16")
+        SCRATCH["ro%d%d" % (_t, _b)] = ("sbuf", [128, 3 * HALF], "bfloat16")
+        if _t < VISITS - 1:
+            SCRATCH["zi%d%d" % (_t, _b)] = ("sbuf", [128, HALF], "bfloat16")
+            SCRATCH["ri%d%d" % (_t, _b)] = ("sbuf", [128, 3 * HALF], "bfloat16")
+            SEMAPHORES.append("az%d%d" % (_t, _b))
+            SEMAPHORES.append("ar%d%d" % (_t, _b))
+
+
+def relays(topo, cores, q):
+    src, dst = cores[q], cores[(q + 1) % len(cores)]
+    c = [h for h in topo.cores_of(src) if h not in cores and topo.die(h) == topo.die(src)
+         and topo.may_write(src, h) and topo.may_write(h, dst)]
+    return c[0], c[1 % len(c)]
+
+
+def relay_program(g, core, T, topo, dst, src, kinds):
+    n_in = len(topo.engines(src, core))
+    n_out = len(topo.engines(core, dst))
+    rid, pid = topo.addr(dst, core)
+    sent = {"z": 0, "r": 0}
+    for t in range(VISITS - 1):
+        for b in range(2):
+            for k in kinds:
+                g.wait_ge(T.sem["a%s%d%d" % (k, t, b)], n_in)
+                buf = T["%si%d%d" % (k, t, b)]
+                g.remote_dma(buf[:], buf[:], T.sem["a%s%d%d" % (k, t, b)], T.sem[k + "sent"], pid, rid, topo.mask(core, dst))
+                sent[k] += n_out
+    for k in kinds:
+        g.wait_ge(T.sem[k + "sent"], sent[k])
+
+
+def rank_program(g, core, T, topo):
+    rank = T.rank_of(core)
+    cores = list(T.cores)
+    if rank is None:
+        for q in range(len(cores)):
+            rl = relays(topo, cores, q)
+            if core in rl:
+                kinds = [k for k, h in zip("zr", rl) if h == core]
+                relay_program(g, core, T, topo, cores[(q + 1) % len(cores)], cores[q], kinds)
+        return
+
+    ops, acc, used = [], {}, {"pi": 0, "pf": 0, "pb": 0, "pu": 0}
+    SIZE = {"pi": 4, "pf": 4, "pb": 2, "pu": 2}
+
+    def alloc(pool, n):
+        lo = used[pool]
+        used[pool] = lo + -(-n // 16) * 16
+        return (pool, lo, lo + n, 1)
+
+    def sub(t, a, b, s=1):
+        return (t[0], t[1] + a, t[1] + b, s)
+
+    def whole(name, n):
+        return (name, 0, n, 1)
+
+    def ap(t, rows=128):
+        buf = T[t[0]]
+        if rows < 128:
+            return buf[0:rows, t[1]:t[2]]
+        return buf[:, t[1]:t[2]] if t[3] == 1 else buf[:, t[1]:t[2]:t[3]]
+
+    def cnt(t):
+        return -(-(t[2] - t[1]) // t[3])
+
+    def size(t):
+        return 4 if t[0][:2] == "ps" else SIZE.get(t[0], 2)
+
+    def op(eng, fns, reads, writes, dur, done=None, lat=0.0, extra=()):
+        me = len(ops)
+        deps = set(extra)
+        for regs, wr in ((reads, False), (writes, True)):
+            for name, lo, hi, _s in regs:
+                bank = name[:2] == "ps"
+                if bank:
+                    lo, hi = 0, 512
+                keep = []
+                for (a, b, o, w_) in acc.get(name, []):
+                    if o != me and a < hi and lo < b and (wr or w_ or bank):
+                        deps.add(o)
+                    if o == me or not ((wr or bank) and lo <= a and b <= hi):
+                        keep.append((a, b, o, w_))
+                keep.append((lo, hi, me, wr or bank))
+                acc[name] = keep
+        ops.append(dict(eng=eng, fns=fns, deps=deps, dur=dur, done=done, lat=lat))
+        return me
+
+    CY, GF = 0.00083, 1.5
+
+    def vd(cyc):
+        return 0.06 + CY * max(64, cyc)
+
+    def fast(*tiles):
+        return 0.5 if all(size(t) == 2 for t in tiles) else 1
+
+    def tt(out, a, b, o):
+        c = 1 if "ps" in (a[0][:2], b[0][:2]) else 2
+        return op("v", [lambda: g.vector.tensor_tensor(ap(out), ap(a), ap(b), o)], [a, b], [out], vd(c * cnt(out)))
+
+    def ts(out, a, s1, o1, s2=None, o2=None):
+        def val(s):
+            return ap(s) if isinstance(s, tuple) else s
+
+        def call():
+            if o2 is None:
+                return g.vector.tensor_scalar(ap(out), ap(a), val(s1), None, o1)
+            return g.vector.tensor_scalar(ap(out), ap(a), val(s1), val(s2), o1, o2)
+        return op("v", [call], [a] + [s for s in (s1, s2) if isinstance(s, tuple)], [out], vd(fast(out, a) * cnt(out)))
+
+    def cp(out, a, rows=128):
+        return op("v", [lambda: g.vector.tensor_copy(ap(out, rows), ap(a, rows))], [a], [out], vd(fast(out, a) * cnt(out)))
+
+    def fill(out, v):
+        return op("v", [lambda: g.vector.memset(ap(out), v)], [], [out], vd(cnt(out) * size(out) / 4))
+
+    def act(out, a, f, scale=1.0, bias=0.0, accum=None):
+        def call():
+            kw = {}
+            if scale != 1.0:
+                kw["scale"] = scale
+            if isinstance(bias, tuple):
+                kw["bias"] = ap(bias)
+            elif bias != 0.0:
+                kw["bias"] = bias
+            if accum is not None:
+                kw["accum_out"] = ap(accum)
+            return g.scalar.activation(ap(out), ap(a), f, **kw)
+        rd = [a] + ([bias] if isinstance(bias, tuple) else [])
+        return op("s", [call], rd, [out] + ([accum] if accum else []), 0.08 + CY * cnt(out))
+
+    def win(a, off):
+        return T[a[0]][:, a[1]:a[2]].indirect(ap(off))
+
+    def gat(eng, out, a, off):
+        n = cnt(out)
+        if eng == "v":
+            return op("v", [lambda: g.vector.tensor_copy(ap(out), win(a, off))], [a, off], [out], 0.05 + CY * GF * n)
+        return op("s", [lambda: g.scalar.activation(ap(out), win(a, off), AF.Copy)], [a, off], [out], 0.065 + CY * GF * n)
+
+    def gat2(split, out, st, a, off, w):
+        if split < w:
+            gat("v", sub(out, 16 * st * split, 16 * st * w, st), a, sub(off, split, w))
+        if split:
+            gat("s", sub(out, 0, 16 * st * split, st), a, sub(off, 0, split))
+
+    def gtt(out, a, off, b, o):
+        return op("v", [lambda: g.vector.tensor_tensor(ap(out), win(a, off), ap(b), o)], [a, off, b], [out],
+                  0.05 + CY * GF * cnt(out))
+
+    def scat(a, off, src):
+        return op("v", [lambda: g.vector.tensor_copy(win(a, off), ap(src))], [src, off], [a], 0.05 + CY * 3.8 * cnt(src))
+
+    def mm(groups, keep_open=False, cont=False, k8=False, m8=False):
+        fns, rd, wr, cyc = [], [], [], 0
+        for out, pairs in groups:
+            for j, (l, r) in enumerate(pairs):
+                o_ = out
+                if len(r) == 2:
+                    o_, r = r
+                start, stop = j == 0 and not cont, j == len(pairs) - 1 and not keep_open
+
+                def call(o_=o_, l=l, r=r, start=start, stop=stop):
+                    return g.tensor.matmul(ap(o_, 8 if m8 else 128), ap(l, 8 if k8 else 128), ap(r, 8 if k8 else 128), start, stop)
+                fns.append(call)
+                rd += [l, r]
+                wr.append(o_)
+                cyc += max(64, cnt(r)) * (4 if size(l) == 4 else 1)
+        return op("t", fns, list(dict.fromkeys(rd)), list(dict.fromkeys(wr)), 0.05 + cyc * 0.00042)
+
+    def gps(fn, rd, wr, dur):
+        return op("g", [fn], rd, wr, dur)
+
+    n_dma = [0]
+
+    def dma(out_ap, in_ap, rd, wr, eng="y", dur=2.5):
+        sem = "dma%d" % n_dma[0]
+        n_dma[0] += 1
+        q = g.sync if eng == "y" else g.scalar
+        return op(eng, [lambda: q.dma_start(out_ap, in_ap)], rd, wr, 0.1, done=(sem, 16), lat=dur)
+
+    xs, dn = whole("xs", W + EXT), whole("dn", ND)
+    zed0, rend0, lend0 = whole("zed0", LANES), whole("rend0", LANES), whole("lend0", LANES)
+    dma(T.zed0[:], T.zed[:], [], [zed0])
+    dma(T.wt0[:], T.wt[:], [], [whole("wt0", 1)], "s")
+    dma(T.kap0[:], T.kap[:], [], [whole("kap0", 1)], "s")
+    dma(T.xs[:, 0:W], T.stock[:], [], [sub(xs, 0, W)], dur=4.0)
+    dma(T.xs[:, W:W + EXT], T.stock[:, 0:EXT], [], [sub(xs, W, W + EXT)])
+    dma(T.rend0[:], T.rend[:], [], [rend0])
+    dma(T.cnt0[:], T.cnt[:], [], [whole("cnt0", LANES)])
+    dma(T.lim0[:], T.lim[:], [], [whole("lim0", 2)])
+    dma(T.dn[:, 0:ND], T.donor[:], [], [dn], dur=3.0)
+    dma(T.lend0[:], T.lend[:], [], [lend0])
+
+    ones = alloc("pb", 128)
+    fill(ones, 1.0)
+    bo1, BO, ID, TRI, TRS = [alloc("pb", 128) for _ in range(5)]
+
+    def sel(out, a, pattern, cmp_, base, cm):
+        gps(lambda: g.affine_select(ap(out), ap(a), pattern, cmp_, 0.0, base, cm), [a], [out], 0.4)
+    sel(bo1, ones, [[-16, 8], [0, 16]], OP.is_ge, 0, 1)
+    sel(BO, bo1, [[16, 8], [0, 16]], OP.is_ge, 15, -1)
+    pidx, q16 = alloc("pi", 1), alloc("pi", 16)
+    gps(lambda: g.iota(ap(pidx), [[0, 1]], 0, 1), [], [pidx], 0.15)
+    gps(lambda: g.iota(ap(q16), [[16, 16]], 0, 0), [], [q16], 0.2)
+    sel(ID, ones, [[-1, 128]], OP.is_equal, 0, 1)
+    mq = alloc("pf", 128)
+    gps(lambda: g.iota(ap(mq), [[1, 16], [0, NQ]], 0, 0, allow_small_or_imprecise_dtypes=True), [], [mq], 0.4)
+    sel(TRI, BO, [[1, 128]], OP.is_ge, 0, -1)
+    sel(TRS, BO, [[1, 128]], OP.is_ge, 1, -1)
+
+    wtf, kapf, kc, k29, k256, nbias, nk0, nk1 = [alloc("pf", 1) for _ in range(8)]
+    ts(wtf, whole("wt0", 1), 0.5, OP.mult)
+    WB = alloc("pb", 128)
+    ts(WB, BO, wtf, OP.mult)
+    EA, FA, WA = alloc("pb", 2048), alloc("pb", 2048), alloc("pb", 2048)
+    fill(WA, 0.0)
+
+    def col8(t, r, k):
+        return sub(t, 128 * r + k, 128 * r + 128, 16)
+    cp(kapf, whole("kap0", 1))
+    kci = alloc("pi", 1)
+    ts(kci, pidx, 15, OP.bitwise_and)
+    cp(kc, kci)
+    ts(k29, kci, 29.0, OP.mult)
+    for r in range(16):
+        cp(col8(WA, r, r), sub(WB, r, 128, 16))
+    zz = {}
+    for b in range(2):
+        zz[b] = alloc("pb", HALF)
+        act(zz[b], sub(zed0, b * HALF, (b + 1) * HALF), AF.Copy, scale=2.0)
+    nID, hID, mB, pB, TRB, BO64, I64 = [alloc("pb", 128) for _ in range(7)]
+    ts(nID, ID, -1.0, OP.mult)
+    ts(hID, ID, -0.5, OP.mult)
+    ts(k256, kci, 256.0, OP.mult)
+    KD1, KD2 = alloc("pb", 128), alloc("pb", 128)
+    ts(KD1, mq, kc, OP.is_equal, kapf, OP.mult)
+    ts(KD2, mq, kc, OP.is_equal, k256, OP.mult)
+    fill(EA, 0.0)
+    for r in range(16):
+        act(col8(EA, r, r), sub(BO, r, 128, 16), AF.Copy)
+    il, l8c, l4c = alloc("pi", 16), alloc("pi", 16), alloc("pi", 16)
+    l32 = alloc("pb", 16)
+    ts(il, q16, kc, OP.add)
+    ts(l32, il, 32.0, OP.mult)
+    ts(l8c, il, 8.0, OP.mult)
+    ts(l4c, il, 4.0, OP.mult)
+    fill(FA, 0.0)
+    for k in range(16):
+        act(col8(FA, k, k), sub(BO, k, 128, 16), AF.Copy, scale=-0.5)
+        if k < 15:
+            act(col8(FA, k, k + 1), sub(BO, k, 128, 16), AF.Copy, scale=0.5)
+    ts(mB, ID, -8192.0, OP.mult)
+    ts(pB, ID, 8192.0, OP.mult)
+    ts(TRB, TRI, 8192.0, OP.mult)
+    ts(BO64, BO, -64.0, OP.mult)
+    ts(I64, ID, 64.0, OP.mult)
+    ts(nk0, kc, -1.0, OP.mult)
+    ts(nk1, kc, -1.0, OP.mult, 1.0, OP.add)
+    ts(nbias, kc, 14.5, OP.is_lt, 2.0, OP.mult)
+    o16 = alloc("pf", 128)
+    fill(o16, 0.0625)
+    cntb, limf, b8b, b8f, nB0 = alloc("pb", LANES), alloc("pf", 2), alloc("pb", 128), alloc("pf", 128), alloc("pb", LANES)
+    cp(cntb, whole("cnt0", LANES), rows=8)
+    cp(limf, whole("lim0", 2), rows=8)
+    gps(lambda: g.affine_select(ap(b8b, 8), ap(ones, 8), [[1, 8], [0, 16]], OP.is_equal, 0.0, 0, -1), [ones], [b8b], 0.4)
+    cp(b8f, b8b, rows=8)
+    mm([(("ps7", 0, LANES, 1), [(b8b, cntb)])], k8=True)
+    act(nB0, ("ps7", 0, LANES, 1), AF.Copy)
+    mm([(("ps7", 0, 2, 1), [(b8f, limf)])], k8=True)
+    thc, sbc = alloc("pf", 1), alloc("pf", 1)
+    act(thc, ("ps7", 0, 1, 1), AF.Copy)
+    act(sbc, ("ps7", 1, 2, 1), AF.Copy, scale=0.5)
+    G8 = alloc("pb", 8)
+    cp(G8, sub(ID, 0, 128, 16))
+
+    H16, w = 16 * HALF, HALF
+    Gb, Hb, ADb, AD2, ZY, REL = [[alloc("pb", n) for _ in range(2)] for n in (H16, H16, H16, H16, 2 * H16, 2 * H16)]
+    for b in range(2):
+        fill(ZY[b], 0.0)
+    par = {}
+
+    def til(pool, n, key, t, b):
+        k = (key, t % 2, b)
+        if k not in par:
+            par[k] = alloc(pool, n)
+        return par[k]
+    A0 = alloc("pf", 1)
+    fill(A0, 0.0)
+    accs = [alloc("pf", 2) for _ in range(2)]
+    state = {b: dict(z2=zz[b], R=sub(rend0, b * w, (b + 1) * w), L=sub(lend0, b * w, (b + 1) * w),
+                     n=sub(nB0, b * w, (b + 1) * w)) for b in range(2)}
+
+    def E(k):
+        return sub(EA, 128 * k, 128 * k + 128)
+
+    def F(k):
+        return sub(FA, 128 * k, 128 * k + 128)
+
+    def ps(bank, a, b):
+        return ("ps%d" % bank, a, b, 1)
+
+    def front(t, b, A):
+        s = state[b]
+        BS, BM = 4 + 2 * b, 5 + 2 * b
+
+        def ti(key, n=w):
+            return til("pi", n, key, t, b)
+        z2 = s["z2"]
+        UW = w + NQ
+        U = ps(BS, 0, UW)
+        mm([(ps(BS, 0, w), [(WB, z2)]),
+            (ps(BS, w, UW), [(sub(WA, 128 * r, 128 * r + 128), sub(z2, r, w, 16)) for r in range(16)])])
+        ui, u, uu, s1, u4 = [ti(k, UW) for k in ("ui", "u", "uu", "s1", "u4")]
+        s2, s3, c = [ti(k) for k in ("s2", "s3", "c")]
+        cl = til("pu", w, "cl", t, b)
+        cp(ui, U)
+        ts(u, ui, 4095, OP.bitwise_and)
+        uA, ul, sA, sl = sub(u, 0, w), sub(u, w, UW), sub(s1, 0, w), sub(s1, w, UW)
+        tt(uu, u, u, OP.mult)
+        ts(s2, uA, kapf, OP.mult, A, OP.add)
+        ts(s1, uu, 5, OP.arith_shift_right)
+        tt(s3, sA, s2, OP.add)
+        ts(c, s3, 2047, OP.bitwise_and)
+        cp(cl, c)
+        gat2(GS[b], Gb[b], 1, sub(xs, 0, W), cl, w)
+        up, pr, pr2 = til("pf", w, "up", t, b), ti("pr"), ti("pr2")
+        hl = til("pu", w, "hl", t, b)
+        ts(up, uA, 32.0, OP.add)
+        tt(pr, s["R"], up, OP.mult)
+        ts(pr2, pr, 5, OP.arith_shift_right, 2047, OP.bitwise_and)
+        ts(hl, pr2, k29, OP.add)
+        gat2(HS[b], Hb[b], 1, xs, hl, w)
+        s1a, x8, l8, b4 = [ti(k, NQ) for k in ("s1a", "x8", "l8", "b4")]
+        l8u = til("pu", NQ, "l8u", t, b)
+        ts(s1a, sl, A, OP.add)
+        ts(x8, ul, 7, OP.bitwise_and)
+        tt(l8, x8, sub(l8c, 0, NQ), OP.add)
+        cp(l8u, l8)
+        ts(u4, u, 3, OP.bitwise_and)
+        tt(b4, sub(u4, w, UW), sub(l4c, b * NQ, (b + 1) * NQ), OP.add)
+        kln, kle = til("pb", w, "kln", t, b), til("pb", w, "kle", t, b)
+        act(kln, s["n"], AF.Relu, bias=nk0)
+        act(kle, s["n"], AF.Relu, bias=nk1)
+        zm = til("pf", w, "zm", t, b)
+        act(zm, z2, AF.Copy, scale=0.5, bias=-0.5)
+        k0 = til("pf", 8 * NQ, "k0", t, b)
+        for mc in range(4):
+            D = 2 * b + mc % 2
+            mm([(ps(D, j * w, (j + 1) * w), [(ID, sub(Gb[b], 4 * mc + j, H16, 16)), (hID, z2)]) for j in range(4)])
+            act(sub(ADb[b], mc * 4 * w, (mc + 1) * 4 * w), ps(D, 0, 512), AF.Abs, scale=4096.0)
+            if mc % 2 == 1:
+                h = mc // 2
+                K = ps(BS if h == 0 else BM, 0, 8 * NQ)
+                mm([(K, [(BO, sub(KD1, 64 * h, 64 * h + 64)), (BO, sub(KD2, 64 * h, 64 * h + 64))]
+                     + [(E(r), sub(ADb[b], h * 8 * w + r, (h + 1) * 8 * w, 16)) for r in range(16)])])
+                if h == 0:
+                    act(k0, K, AF.Copy)
+        t1, t2, t3 = [til("pf", n, "tm%d" % n, t, b) for n in (64, 32, 16)]
+        vi, ka, pa, pc, cd, cx = [ti(k, NQ) for k in ("vi", "ka", "pa", "pc", "cd", "cx")]
+        cdu, cxu = til("pu", NQ, "cdu", t, b), til("pu", NQ, "cxu", t, b)
+        tt(t1, ps(BM, 0, 64), k0, OP.min)
+        tt(t2, sub(t1, 0, 32), sub(t1, 32, 64), OP.min)
+        tt(t3, sub(t2, 0, 16), sub(t2, 16, 32), OP.min)
+        tt(vi, sub(t3, 0, 8), sub(t3, 8, 16), OP.min)
+        ts(ka, vi, 255, OP.bitwise_and)
+        tt(pa, ka, ul, OP.mult)
+        tt(pc, pa, s1a, OP.add)
+        ts(cd, pc, 1023, OP.bitwise_and)
+        cp(cdu, cd)
+        P, P2 = ti("P"), ti("P2")
+        yl = til("pu", w, "yl", t, b)
+        gtt(P, dn, cdu, up, OP.mult)
+        ts(P2, P, 5, OP.arith_shift_right, 2047, OP.bitwise_and)
+        ts(yl, P2, k29, OP.add)
+        ts(cx, pc, 2047, OP.bitwise_and)
+        cp(cxu, cx)
+        Dk, xc = til("pb", w, "Dk", t, b), til("pb", w, "xc", t, b)
+        for h in range(2):
+            gat(YE[b][h], sub(ZY[b], h * H16, (h + 1) * H16, 2), xs, sub(yl, h * w // 2, (h + 1) * w // 2))
+        gat("s", Dk, dn, cdu)
+        gat("s", xc, sub(xs, 0, W), cxu)
+        s.update(kln=kln, kle=kle, zm=zm, Dk=Dk, xc=xc, u3=sub(u4, 0, w), l8u=l8u, b4=b4)
+
+    def tail(t, b):
+        s = state[b]
+        BS, BM = 4 + 2 * b, 5 + 2 * b
+        z, H, rel = ZY[b], Hb[b], REL[b]
+
+        def tb(key):
+            return til("pb", w, key, t, b)
+        J, M, e = ps(BS, 0, w), ps(BM, 0, w), w // 2
+        for h in range(2):
+            lo, hi = h * H16, (h + 1) * H16
+            op("v", [lambda lo=lo, hi=hi: g.vector.tensor_tensor_scan(
+                ap(sub(rel, lo, hi - 1)), ap(sub(z, lo + 1, hi)), ap(sub(z, lo, hi - 1)), 0.0, OP.subtract, OP.max)],
+               [sub(z, lo, hi)], [sub(rel, lo, hi - 1)], vd(0.5 * H16))
+            for kq in range(2):
+                D = 2 * b + kq
+                mm([(ps(D, j * e, (j + 1) * e), [(ID, sub(z, lo + 2 * (8 * kq + j), hi, 32)),
+                                                 (nID, sub(H, lo // 2 + 8 * kq + j, hi // 2, 16))]) for j in range(8)])
+                act(sub(AD2[b], lo // 2 + kq * 512, lo // 2 + (kq + 1) * 512), ps(D, 0, 512), AF.Abs)
+            jh, mh = sub(J, h * e, (h + 1) * e), sub(M, h * e, (h + 1) * e)
+            mm([(jh, ([(mB, (J, s["kle"]))] if h == 0 else [])
+                 + [(F(k), sub(z, lo + 2 * k, hi, 32)) for k in range(16)]
+                 + [(E(k), sub(rel, lo + 2 * k - 1, hi - 1, 32)) for k in range(1, 16)])], keep_open=h == 0, cont=h == 1)
+            mm([(mh, ([(pB, (M, s["kln"]))] if h == 0 else [])
+                 + [(E(k), sub(AD2[b], lo // 2 + k * e, lo // 2 + (k + 1) * e)) for k in range(16)])], keep_open=True, cont=h == 1)
+        jm, me, ne = tb("jm"), tb("me"), tb("ne")
+        ts(jm, J, sbc, OP.is_gt)
+        mm([(M, [(TRB, jm)])], cont=True)
+        ts(me, M, thc, OP.is_le)
+        mm([(ps(BS, 0, w), [(TRI, me), (TRS, jm)])])
+        act(ne, ps(BS, 0, w), AF.Relu, scale=-2.0, bias=nbias)
+        mm([(ps(BM, 0, NQ), [(ID, sub(l32, 0, NQ))] + [(E(r), sub(ne, r, w, 16)) for r in range(16)])])
+        yel = til("pu", NQ, "yel", t, b)
+        cp(yel, ps(BM, 0, NQ))
+        sz = til("pf", w, "sz", t, b)
+        zo = whole("zo%d%d" % (t, b), w)
+        gtt(sz, z, yel, s["zm"], OP.add)
+        ts(zo, sz, MAGIC, OP.add, MAGIC, OP.subtract)
+        if t < VISITS - 1:
+            send("z", t, b, zo)
+        sx, sx2 = til("pi", w, "sx", t, b), til("pi", w, "sx2", t, b)
+        gtt(sx, z, yel, s["xc"], OP.add)
+        ts(sx2, sx, 1, OP.arith_shift_right)
+        mm([(ps(BS, 0, w), [(BO, me)]), (ps(BS, w, 2 * w), [(BO, jm), (BO64, me)]), (ps(BS, 2 * w, 3 * w), [(TRI, me)]),
+            (ps(BS, 3 * w, 4 * w), [(TRI, jm), (I64, s["kln"])])])
+        an, nm2, m1, dn1, nd6 = tb("an"), tb("nm2"), tb("m1"), tb("dn1"), tb("nd6")
+        act(an, ps(BS, 0, w), AF.Sign, accum=sub(accs[t % 2], b, b + 1))
+        act(m1, ps(BS, 3 * w, 4 * w), AF.Relu, scale=-1.0, bias=1.0)
+        act(nm2, ps(BS, 2 * w, 3 * w), AF.Relu, scale=-1.0, bias=1.0)
+        ts(dn1, ps(BS, w, 2 * w), 0.5, OP.is_lt)
+        act(nd6, dn1, AF.Copy, scale=-64.0, bias=64.0)
+        s.update(sx2=sx2, dn1=dn1, nd6=nd6, m1=m1, nm2=nm2)
+
+    def count(t):
+        A = ps(6, 0, 1)
+        mm([(A, [(o16, sub(accs[t % 2], b, b + 1)) for b in range(2)])])
+        ac = til("pf", 1, "A", t, 0)
+        act(ac, A, AF.Copy)
+        return ac
+
+    def writes_x(t, b):
+        scat(sub(xs, b * W // 2, (b + 1) * W // 2), state[b]["l8u"], state[b]["sx2"])
+        if b == 0 and t < VISITS - 1:
+            cp(sub(xs, W, W + EXT), sub(xs, 0, EXT))
+
+    def update(t, b):
+        s = state[b]
+        BS, BM = 4 + 2 * b, 5 + 2 * b
+
+        def tb(key):
+            return til("pb", w, key, t, b)
+        tl, x, x2, Q, Q2 = [tb(k) for k in ("tl", "x", "x2", "Q", "Q2")]
+        L, R = s["L"], s["R"]
+        mm([(ps(BM, 0, w), [(ID, s["Dk"]), (nID, L)]), (ps(BM, w, 2 * w), [(ID, s["n"]), (BO, s["m1"])])])
+        tt(tl, s["m1"], ps(BM, 0, w), OP.mult)
+        tt(x, s["u3"], ps(BM, w, 2 * w), OP.subtract)
+        tt(x2, x, s["dn1"], OP.mult)
+        mm([(ps(BM, 0, w), [(ID, tl), (ID, L), (nID, R)])])
+        tt(Q, s["nm2"], ps(BM, 0, w), OP.mult)
+        tt(Q2, Q, s["dn1"], OP.mult)
+        mm([(ps(BM, 0, w), [(ID, R), (ID, Q2)]), (ps(BM, w, 2 * w), [(ID, s["n"]), (BO, s["m1"]), (ID, x2), (ID, s["dn1"])]),
+            (ps(BM, 2 * w, 3 * w), [(ID, R), (ID, Q)])])
+        ro = whole("ro%d%d" % (t, b), 3 * w)
+        act(ro, ps(BM, 0, 3 * w), AF.Copy)
+        if t < VISITS - 1:
+            send("r", t, b, ro)
+        mm([(ps(BS, 0, NQ), [(E(r), sub(s["nd6"], r, w, 16)) for r in range(16)])])
+        dl, dlu = til("pi", NQ, "dl", t, b), til("pu", NQ, "dlu", t, b)
+        tt(dl, s["b4"], ps(BS, 0, NQ), OP.add)
+        cp(dlu, dl)
+        scat(whole("dn", 2 * ND), dlu, sub(ro, 2 * w, 3 * w))
+
+    snt = {"z": 0, "r": 0}
+
+    def send(k, t, b, tile):
+        dst = relays(topo, cores, rank)["zr".index(k)]
+        rid, pid = topo.addr(dst, core)
+        m = topo.mask(core, dst)
+        snt[k] += len(topo.engines(core, dst))
+        name = "%s%d%d" % (k, t, b)
+        o = op("g", [lambda: g.remote_dma(T[k + "i" + name[1:]][:], ap(tile), T.sem["a" + name], T.sem[k + "sent"], pid, rid, m)],
+               [tile], [], 1.0, done=(k + "sent", 0))
+        n = len(topo.engines(relays(topo, cores, (rank - 1) % len(cores))["zr".index(k)], core))
+        op(None, [], [], [whole(k + "i" + name[1:], cnt(tile))], 0.0, done=("a" + name, n), lat=4.0, extra=(o,))
+
+    A = A0
+    for t in range(VISITS):
+        for b in range(2):
+            front(t, b, A)
+        for b in range(2):
+            tail(t, b)
+        A = count(t)
+        for b in range(2):
+            writes_x(t, b)
+        for b in range(2):
+            update(t, b)
+        for b in range(2):
+            if t < VISITS - 1:
+                r = whole("ri%d%d" % (t, b), 3 * w)
+                state[b] = dict(z2=whole("zi%d%d" % (t, b), w), R=sub(r, 0, w), n=sub(r, w, 2 * w), L=sub(r, 2 * w, 3 * w))
+            else:
+                zo, r = whole("zo%d%d" % (t, b), w), whole("ro%d%d" % (t, b), 3 * w)
+                lo, hi = b * w, (b + 1) * w
+                act(sub(whole("yz0", LANES), lo, hi), zo, AF.Copy, scale=0.5)
+                dma(T.yz[:, lo:hi], T.yz0[:, lo:hi], [("yz0", lo, hi, 1)], [])
+                mm([(ps(4, 0, w), [(G8, sub(r, w, 2 * w))])], m8=True)
+                op("s", [lambda lo=lo, hi=hi: g.scalar.activation(T.yn0[:, lo:hi], T.ps4[0:8, 0:w], AF.Copy)],
+                   [ps(4, 0, w)], [("yn0", lo, hi, 1)], 0.2)
+                dma(T.yr[:, lo:hi], ap(sub(r, 0, w)), [r], [])
+                dma(T.yl[:, lo:hi], ap(sub(r, 2 * w, 3 * w)), [r], [])
+    dma(T.yn[:], T.yn0[:], [("yn0", 0, LANES, 1)], [])
+    for b in range(2):
+        lo, hi = b * W // 2, (b + 1) * W // 2
+        dma(T.yx[:, lo:hi], T.xs[:, lo:hi], [sub(xs, lo, hi)], [])
+    dma(T.yd[:], T.dn[:, 0:ND], [dn], [])
+
+    N = len(ops)
+    succ = [[] for _ in range(N)]
+    for i, o in enumerate(ops):
+        for d in o["deps"]:
+            succ[d].append(i)
+    prio = [0.0] * N
+    for i in range(N - 1, -1, -1):
+        prio[i] = ops[i]["dur"] + ops[i]["lat"] + max([prio[j] for j in succ[i]] + [0.0])
+    left = [len(o["deps"]) for o in ops]
+    ready = {e: [] for e in ("v", "s", "t", "g", "y", None)}
+    avail = [0.0] * N
+    free = {e: 0.0 for e in ready}
+    for i in range(N):
+        if left[i] == 0:
+            ready[ops[i]["eng"]].append(i)
+    order = []
+    while len(order) < N:
+        best = None
+        for e, lst in ready.items():
+            if lst:
+                st = max(free[e], min(avail[i] for i in lst)) if e is not None else min(avail[i] for i in lst)
+                if best is None or st < best[0]:
+                    best = (st, e)
+        st, e = best
+        i = max((j for j in ready[e] if avail[j] <= st + 1e-9), key=lambda j: prio[j])
+        ready[e].remove(i)
+        end = st + ops[i]["dur"]
+        if e is not None:
+            free[e] = end
+        order.append((st, i))
+        for j in succ[i]:
+            left[j] -= 1
+            avail[j] = max(avail[j], end + ops[i]["lat"] + 0.06)
+            if left[j] == 0:
+                ready[ops[j]["eng"]].append(j)
+
+    QUEUE = {"v": g.vector, "s": g.scalar, "t": g.tensor, "g": g, "y": g.sync}
+    SEM = {"v": "sv", "s": "ss", "t": "st", "g": "sg"}
+    made = {k: 0 for k in SEM.values()}
+    know = {e: {} for e in QUEUE}
+    final = {}
+    for st, i in order:
+        o = ops[i]
+        e = o["eng"]
+        if e is None:
+            o["clock"], o["mark"] = {}, o["done"]
+            final[o["done"][0]] = o["done"][1]
+            continue
+        kn = know[e]
+        need = {}
+        for d in o["deps"]:
+            m = ops[d]["mark"]
+            if m is not None and kn.get(m[0], 0) < m[1]:
+                need[m[0]] = max(need.get(m[0], 0), m[1])
+        for d in sorted(o["deps"], reverse=True):
+            m = ops[d]["mark"]
+            if m is None or need.get(m[0], 0) != m[1]:
+                continue
+            for k, v in ops[d]["clock"].items():
+                if k != m[0] and k in need and need[k] <= v:
+                    need.pop(k)
+        for k in need:
+            QUEUE[e].wait_ge(T.sem[k], need[k])
+        for d in o["deps"]:
+            m = ops[d]["mark"]
+            if m is not None:
+                kn[m[0]] = max(kn.get(m[0], 0), m[1])
+                for k, v in ops[d]["clock"].items():
+                    kn[k] = max(kn.get(k, 0), v)
+        o["clock"] = dict(kn)
+        for f in o["fns"]:
+            ins = f()
+        if o["done"] is None:
+            made[SEM[e]] += 1
+            ins.then_inc(T.sem[SEM[e]], 1)
+            o["mark"] = (SEM[e], made[SEM[e]])
+        elif o["done"][1] == 16:
+            ins.then_inc(T.sem[o["done"][0]], 16)
+            o["mark"] = o["done"]
+            final[o["done"][0]] = 16
+        else:
+            o["mark"] = None
+    for k in SEM.values():
+        g.wait_ge(T.sem[k], made[k])
+    for k, v in final.items():
+        g.wait_ge(T.sem[k], v)
+    for k in ("z", "r"):
+        g.wait_ge(T.sem[k + "sent"], snt[k])

@@ -6,7 +6,23 @@ LANES, HALF, NQ, VISITS = 256, 128, 8, 5
 W, EXT, ND = 2048, 448, 1024
 MAGIC = 25165824.0
 
-GS, HS, YE = (128, 0), (128, 64), ("ss", "sv")
+GS, HS, YE = (128, 32), (64, -1), ("vs", "vs")
+NUDGE = {
+    "c": [-10, 0, -7, 0, -6, 0, 5, 4, 0, -4, 0, -5, 0, 1, 0, 4, -6, -2, 0, 2, 2, 1, 3, -4, 9, -4, 0, 1, 0, -6, -6, -3, 2, 3, 1, 1,
+          -2, 2, 2, 3, -1, 13, 10, -1, 3, 0, -10, 0, -8, 0, 0, 4, -2, 3, 0, -8, -3, -7, 8, 4, -1, 0, 0, -7, 16, 0, 0, -11, -9,
+          -1, 5, 1, 4, 11, -2, 0, 0, -4, 5, 7, -5, 2, -7, 0, 0, -1, 2, 2, -10, 0, -5, 0, 12, 6, -7, 0, 1, 0, -11, -5, 2, 2, 0,
+          -8, 0, 3, 6, -1, 0, 10, -4, 0, -3, 1, 4, 4, -5, 1, 3, -5, -7, -5, 8, -2, -8, -1],
+    "e0": [5, 0, -1, -2, 0, 6, -2, 0, 0, 1, -1, 9, -5],
+    "f0": [7, -1, 0, 1, 0, 5, 0, 8, 0, -2, 2, 6, -4, -2, 2, 16, -6, -1, 10, -4, -5, -3, 0, 0, 4, 6, 5, 1, 5, 8, 15, -1, -2, 10,
+           1, -5, 0, 2, -3, 2, 9, -6, 0, 0, 0, -9, 0, -1, 0, -9, 14, -3],
+    "f1": [5, 1, 0, 10, 3, 0, 0, 4, -14, -6, -5, 0, -10, 6, -7, -10, -7, -5, -8, -13, -3, 0, -2, 6, -3, -1, 0, -3, -3, -9, 5, 11,
+           2, 0, 12, 0, 1, -7, -10, -4, 0, -3, 0, 7, -2, 0, -1, -8, -6, 3, 7],
+    "t0": [0, -14, -3, 1, 2, -7, -7, 0, 2, 0, 0, -7, -4, 1, -3, -2, 0, 0, -9, 4, 0, 4, -3, -8, -4, 0, 0, 15, 8, -3, -10, 2],
+    "t1": [-1, 5, 3, -2, 0, -7, -4, -1, 10, 2, 4, 2, 0, 0, 0, 0, -1, 5, 0, 1, 0, 9, -3, 0, -3, 9, 0, 3],
+    "u0": [11, 14, 5, 4, 0, 0, 12, 11, -4, -6, -16, 0, 0, 9],
+    "u1": [5, 11, 5, 0, 0, 1, 2, 4, 2, 2, 14, 2, -3, -2],
+    "w0": [9, -8, -9, -4],
+}
 
 SCRATCH = {
     "pi": ("sbuf", [128, 8448], "int32"), "pf": ("sbuf", [128, 3072], "float32"),
@@ -93,8 +109,12 @@ def rank_program(g, core, T, topo):
     def size(t):
         return 4 if t[0][:2] == "ps" else SIZE.get(t[0], 2)
 
+    stage, seq = ["c"], {}
+
     def op(eng, fns, reads, writes, dur, done=None, lat=0.0, extra=()):
         me = len(ops)
+        place = seq[stage[0]] = seq.get(stage[0], -1) + 1
+        nudge = NUDGE.get(stage[0][:2], [])
         deps = set(extra)
         for regs, wr in ((reads, False), (writes, True)):
             for name, lo, hi, _s in regs:
@@ -109,7 +129,8 @@ def rank_program(g, core, T, topo):
                         keep.append((a, b, o, w_))
                 keep.append((lo, hi, me, wr or bank))
                 acc[name] = keep
-        ops.append(dict(eng=eng, fns=fns, deps=deps, dur=dur, done=done, lat=lat))
+        ops.append(dict(eng=eng, fns=fns, deps=deps, dur=dur, done=done, lat=lat, cls=(stage[0][:2], place),
+                        bias=nudge[place] if place < len(nudge) else 0))
         return me
 
     CY, GF = 0.00083, 1.5
@@ -235,7 +256,7 @@ def rank_program(g, core, T, topo):
     sel(TRI, BO, [[1, 128]], OP.is_ge, 0, -1)
     sel(TRS, BO, [[1, 128]], OP.is_ge, 1, -1)
 
-    wtf, kapf, kc, k29, k256, nbias, nk0, nk1 = [alloc("pf", 1) for _ in range(8)]
+    wtf, kapf, kc, k29, k256, nbias = [alloc("pf", 1) for _ in range(6)]
     ts(wtf, whole("wt0", 1), 0.5, OP.mult)
     WB = alloc("pb", 128)
     ts(WB, BO, wtf, OP.mult)
@@ -250,12 +271,15 @@ def rank_program(g, core, T, topo):
     cp(kc, kci)
     ts(k29, kci, 29.0, OP.mult)
     for r in range(16):
-        cp(col8(WA, r, r), sub(WB, r, 128, 16))
+        if r % 2:
+            act(col8(WA, r, r), sub(WB, r, 128, 16), AF.Copy)
+        else:
+            cp(col8(WA, r, r), sub(WB, r, 128, 16))
     zz = {}
     for b in range(2):
         zz[b] = alloc("pb", HALF)
         act(zz[b], sub(zed0, b * HALF, (b + 1) * HALF), AF.Copy, scale=2.0)
-    nID, hID, mB, pB, TRB, BO64, I64 = [alloc("pb", 128) for _ in range(7)]
+    nID, hID, mB, pB, TRB, BOM, I64, pS, nS = [alloc("pb", 128) for _ in range(9)]
     ts(nID, ID, -1.0, OP.mult)
     ts(hID, ID, -0.5, OP.mult)
     ts(k256, kci, 256.0, OP.mult)
@@ -265,8 +289,9 @@ def rank_program(g, core, T, topo):
     fill(EA, 0.0)
     for r in range(16):
         act(col8(EA, r, r), sub(BO, r, 128, 16), AF.Copy)
-    il, l8c, l4c = alloc("pi", 16), alloc("pi", 16), alloc("pi", 16)
-    l32 = alloc("pb", 16)
+    il, l8c = alloc("pi", 16), alloc("pi", 16)
+    l32, l4c, neg = alloc("pb", 16), alloc("pb", 16), alloc("pb", NQ)
+    fill(neg, -1.0)
     ts(il, q16, kc, OP.add)
     ts(l32, il, 32.0, OP.mult)
     ts(l8c, il, 8.0, OP.mult)
@@ -276,13 +301,14 @@ def rank_program(g, core, T, topo):
         act(col8(FA, k, k), sub(BO, k, 128, 16), AF.Copy, scale=-0.5)
         if k < 15:
             act(col8(FA, k, k + 1), sub(BO, k, 128, 16), AF.Copy, scale=0.5)
-    ts(mB, ID, -8192.0, OP.mult)
+    fill(sub(mB, 0, 1), 0.0)
+    ts(sub(mB, 1, 128), sub(ID, 0, 127), -8192.0, OP.mult)
     ts(pB, ID, 8192.0, OP.mult)
     ts(TRB, TRI, 8192.0, OP.mult)
-    ts(BO64, BO, -64.0, OP.mult)
+    ts(BOM, BO, -1048576.0, OP.mult)
+    ts(pS, ID, 0.015625, OP.mult)
+    ts(nS, ID, -0.015625, OP.mult)
     ts(I64, ID, 64.0, OP.mult)
-    ts(nk0, kc, -1.0, OP.mult)
-    ts(nk1, kc, -1.0, OP.mult, 1.0, OP.add)
     ts(nbias, kc, 14.5, OP.is_lt, 2.0, OP.mult)
     o16 = alloc("pf", 128)
     fill(o16, 0.0625)
@@ -292,13 +318,13 @@ def rank_program(g, core, T, topo):
     gps(lambda: g.affine_select(ap(b8b, 8), ap(ones, 8), [[1, 8], [0, 16]], OP.is_equal, 0.0, 0, -1), [ones], [b8b], 0.4)
     cp(b8f, b8b, rows=8)
     mm([(("ps7", 0, LANES, 1), [(b8b, cntb)])], k8=True)
-    act(nB0, ("ps7", 0, LANES, 1), AF.Copy)
+    ts(nB0, ("ps7", 0, LANES, 1), kc, OP.is_gt)
     mm([(("ps7", 0, 2, 1), [(b8f, limf)])], k8=True)
     thc, sbc = alloc("pf", 1), alloc("pf", 1)
-    act(thc, ("ps7", 0, 1, 1), AF.Copy)
-    act(sbc, ("ps7", 1, 2, 1), AF.Copy, scale=0.5)
+    act(thc, ("ps7", 0, 1, 1), AF.Copy, bias=1.0)
+    act(sbc, ("ps7", 1, 2, 1), AF.Copy, scale=-1.0)
     G8 = alloc("pb", 8)
-    cp(G8, sub(ID, 0, 128, 16))
+    cp(G8, sub(BO, 0, 128, 16))
 
     H16, w = 16 * HALF, HALF
     Gb, Hb, ADb, AD2, ZY, REL = [[alloc("pb", n) for _ in range(2)] for n in (H16, H16, H16, H16, 2 * H16, 2 * H16)]
@@ -337,8 +363,10 @@ def rank_program(g, core, T, topo):
         U = ps(BS, 0, UW)
         mm([(ps(BS, 0, w), [(WB, z2)]),
             (ps(BS, w, UW), [(sub(WA, 128 * r, 128 * r + 128), sub(z2, r, w, 16)) for r in range(16)])])
-        ui, u, uu, s1, u4 = [ti(k, UW) for k in ("ui", "u", "uu", "s1", "u4")]
-        s2, s3, c = [ti(k) for k in ("s2", "s3", "c")]
+        ui, u, uu, s1 = [ti(k, UW) for k in ("ui", "u", "uu", "s1")]
+        u4 = ti("u4")
+        s3, c = ti("s3"), ti("c")
+        s2 = ps(BS, 256, 256 + w)
         cl = til("pu", w, "cl", t, b)
         cp(ui, U)
         ts(u, ui, 4095, OP.bitwise_and)
@@ -356,18 +384,17 @@ def rank_program(g, core, T, topo):
         tt(pr, s["R"], up, OP.mult)
         ts(pr2, pr, 5, OP.arith_shift_right, 2047, OP.bitwise_and)
         ts(hl, pr2, k29, OP.add)
-        gat2(HS[b], Hb[b], 1, xs, hl, w)
-        s1a, x8, l8, b4 = [ti(k, NQ) for k in ("s1a", "x8", "l8", "b4")]
+        if HS[b] >= 0:
+            gat2(HS[b], Hb[b], 1, xs, hl, w)
+        s1a, x8, l8 = [ti(k, NQ) for k in ("s1a", "x8", "l8")]
         l8u = til("pu", NQ, "l8u", t, b)
         ts(s1a, sl, A, OP.add)
         ts(x8, ul, 7, OP.bitwise_and)
         tt(l8, x8, sub(l8c, 0, NQ), OP.add)
         cp(l8u, l8)
-        ts(u4, u, 3, OP.bitwise_and)
-        tt(b4, sub(u4, w, UW), sub(l4c, b * NQ, (b + 1) * NQ), OP.add)
-        kln, kle = til("pb", w, "kln", t, b), til("pb", w, "kle", t, b)
-        act(kln, s["n"], AF.Relu, bias=nk0)
-        act(kle, s["n"], AF.Relu, bias=nk1)
+        ts(u4, uA, 3, OP.bitwise_and)
+        ku = til("pb", w, "ku", t, b)
+        ts(ku, u4, kc, OP.is_ge)
         zm = til("pf", w, "zm", t, b)
         act(zm, z2, AF.Copy, scale=0.5, bias=-0.5)
         k0 = til("pf", 8 * NQ, "k0", t, b)
@@ -406,12 +433,13 @@ def rank_program(g, core, T, topo):
             gat(YE[b][h], sub(ZY[b], h * H16, (h + 1) * H16, 2), xs, sub(yl, h * w // 2, (h + 1) * w // 2))
         gat("s", Dk, dn, cdu)
         gat("s", xc, sub(xs, 0, W), cxu)
-        s.update(kln=kln, kle=kle, zm=zm, Dk=Dk, xc=xc, u3=sub(u4, 0, w), l8u=l8u, b4=b4)
+        s.update(hl=hl, zm=zm, Dk=Dk, xc=xc, ku=ku, l8u=l8u)
 
     def tail(t, b):
         s = state[b]
         BS, BM = 4 + 2 * b, 5 + 2 * b
         z, H, rel = ZY[b], Hb[b], REL[b]
+        fused = HS[b] < 0
 
         def tb(key):
             return til("pb", w, key, t, b)
@@ -421,21 +449,25 @@ def rank_program(g, core, T, topo):
             op("v", [lambda lo=lo, hi=hi: g.vector.tensor_tensor_scan(
                 ap(sub(rel, lo, hi - 1)), ap(sub(z, lo + 1, hi)), ap(sub(z, lo, hi - 1)), 0.0, OP.subtract, OP.max)],
                [sub(z, lo, hi)], [sub(rel, lo, hi - 1)], vd(0.5 * H16))
-            for kq in range(2):
+            if fused:
+                gtt(sub(H, lo // 2, hi // 2), xs, sub(s["hl"], h * e, (h + 1) * e), sub(z, lo, hi, 2), OP.subtract)
+                act(sub(AD2[b], lo // 2, hi // 2), sub(H, lo // 2, hi // 2), AF.Abs)
+            for kq in range(0 if fused else 2):
                 D = 2 * b + kq
                 mm([(ps(D, j * e, (j + 1) * e), [(ID, sub(z, lo + 2 * (8 * kq + j), hi, 32)),
                                                  (nID, sub(H, lo // 2 + 8 * kq + j, hi // 2, 16))]) for j in range(8)])
                 act(sub(AD2[b], lo // 2 + kq * 512, lo // 2 + (kq + 1) * 512), ps(D, 0, 512), AF.Abs)
             jh, mh = sub(J, h * e, (h + 1) * e), sub(M, h * e, (h + 1) * e)
-            mm([(jh, ([(mB, (J, s["kle"]))] if h == 0 else [])
+            mm([(jh, ([(mB, (J, s["n"]))] if h == 0 else [])
                  + [(F(k), sub(z, lo + 2 * k, hi, 32)) for k in range(16)]
                  + [(E(k), sub(rel, lo + 2 * k - 1, hi - 1, 32)) for k in range(1, 16)])], keep_open=h == 0, cont=h == 1)
-            mm([(mh, ([(pB, (M, s["kln"]))] if h == 0 else [])
-                 + [(E(k), sub(AD2[b], lo // 2 + k * e, lo // 2 + (k + 1) * e)) for k in range(16)])], keep_open=True, cont=h == 1)
+            mm([(mh, ([(pB, (M, s["n"]))] if h == 0 else [])
+                 + [(E(k), sub(AD2[b], lo // 2 + k, hi // 2, 16) if fused else
+                     sub(AD2[b], lo // 2 + k * e, lo // 2 + (k + 1) * e)) for k in range(16)])], keep_open=True, cont=h == 1)
         jm, me, ne = tb("jm"), tb("me"), tb("ne")
-        ts(jm, J, sbc, OP.is_gt)
+        act(jm, J, AF.Relu, scale=2.0, bias=sbc)
         mm([(M, [(TRB, jm)])], cont=True)
-        ts(me, M, thc, OP.is_le)
+        act(me, M, AF.Relu, scale=-1.0, bias=thc)
         mm([(ps(BS, 0, w), [(TRI, me), (TRS, jm)])])
         act(ne, ps(BS, 0, w), AF.Relu, scale=-2.0, bias=nbias)
         mm([(ps(BM, 0, NQ), [(ID, sub(l32, 0, NQ))] + [(E(r), sub(ne, r, w, 16)) for r in range(16)])])
@@ -450,15 +482,14 @@ def rank_program(g, core, T, topo):
         sx, sx2 = til("pi", w, "sx", t, b), til("pi", w, "sx2", t, b)
         gtt(sx, z, yel, s["xc"], OP.add)
         ts(sx2, sx, 1, OP.arith_shift_right)
-        mm([(ps(BS, 0, w), [(BO, me)]), (ps(BS, w, 2 * w), [(BO, jm), (BO64, me)]), (ps(BS, 2 * w, 3 * w), [(TRI, me)]),
-            (ps(BS, 3 * w, 4 * w), [(TRI, jm), (I64, s["kln"])])])
-        an, nm2, m1, dn1, nd6 = tb("an"), tb("nm2"), tb("m1"), tb("dn1"), tb("nd6")
+        mm([(ps(BS, 0, w), [(BO, me)]), (ps(BS, w, 2 * w), [(BO, jm), (BOM, me)]), (ps(BS, 2 * w, 3 * w), [(TRI, me)]),
+            (ps(BS, 3 * w, 4 * w), [(TRI, jm), (I64, s["n"])])])
+        an, nm2, m1, nd6 = tb("an"), tb("nm2"), tb("m1"), tb("nd6")
         act(an, ps(BS, 0, w), AF.Sign, accum=sub(accs[t % 2], b, b + 1))
         act(m1, ps(BS, 3 * w, 4 * w), AF.Relu, scale=-1.0, bias=1.0)
         act(nm2, ps(BS, 2 * w, 3 * w), AF.Relu, scale=-1.0, bias=1.0)
-        ts(dn1, ps(BS, w, 2 * w), 0.5, OP.is_lt)
-        act(nd6, dn1, AF.Copy, scale=-64.0, bias=64.0)
-        s.update(sx2=sx2, dn1=dn1, nd6=nd6, m1=m1, nm2=nm2)
+        ts(nd6, ps(BS, w, 2 * w), 0.5, OP.is_gt, 64.0, OP.mult)
+        s.update(sx2=sx2, nd6=nd6, m1=m1, nm2=nm2)
 
     def count(t):
         A = ps(6, 0, 1)
@@ -478,25 +509,28 @@ def rank_program(g, core, T, topo):
 
         def tb(key):
             return til("pb", w, key, t, b)
-        tl, x, x2, Q, Q2 = [tb(k) for k in ("tl", "x", "x2", "Q", "Q2")]
+        tl, Q, Q2 = [tb(k) for k in ("tl", "Q", "Q2")]
+        r3 = til("pb", 4 * w, "r3", t, b)
         L, R = s["L"], s["R"]
-        mm([(ps(BM, 0, w), [(ID, s["Dk"]), (nID, L)]), (ps(BM, w, 2 * w), [(ID, s["n"]), (BO, s["m1"])])])
+        mm([(ps(BM, 0, w), [(ID, s["Dk"]), (nID, L)])])
+        mm([(ps(BS, 0, w), [(nID, ones), (ID, s["n"]), (ID, s["m1"]), (pS, s["nd6"])]),
+            (ps(BS, w, 2 * w), [(ID, s["ku"]), (nS, s["nd6"])]), (ps(BS, 2 * w, 3 * w), [(ID, s["nm2"]), (nS, s["nd6"])]),
+            (ps(BS, 3 * w, 4 * w), [(ID, s["ku"]), (ID, s["nd6"])])])
+        act(r3, ps(BS, 0, 4 * w), AF.Relu)
         tt(tl, s["m1"], ps(BM, 0, w), OP.mult)
-        tt(x, s["u3"], ps(BM, w, 2 * w), OP.subtract)
-        tt(x2, x, s["dn1"], OP.mult)
         mm([(ps(BM, 0, w), [(ID, tl), (ID, L), (nID, R)])])
         tt(Q, s["nm2"], ps(BM, 0, w), OP.mult)
-        tt(Q2, Q, s["dn1"], OP.mult)
-        mm([(ps(BM, 0, w), [(ID, R), (ID, Q2)]), (ps(BM, w, 2 * w), [(ID, s["n"]), (BO, s["m1"]), (ID, x2), (ID, s["dn1"])]),
+        tt(Q2, sub(r3, 2 * w, 3 * w), ps(BM, 0, w), OP.mult)
+        mm([(ps(BM, 0, w), [(ID, R), (ID, Q2)]), (ps(BM, w, 2 * w), [(ID, sub(r3, 0, w)), (ID, sub(r3, w, 2 * w))]),
             (ps(BM, 2 * w, 3 * w), [(ID, R), (ID, Q)])])
         ro = whole("ro%d%d" % (t, b), 3 * w)
         act(ro, ps(BM, 0, 3 * w), AF.Copy)
         if t < VISITS - 1:
             send("r", t, b, ro)
-        mm([(ps(BS, 0, NQ), [(E(r), sub(s["nd6"], r, w, 16)) for r in range(16)])])
-        dl, dlu = til("pi", NQ, "dl", t, b), til("pu", NQ, "dlu", t, b)
-        tt(dl, s["b4"], ps(BS, 0, NQ), OP.add)
-        cp(dlu, dl)
+        mm([(ps(BS, 0, NQ), [(ID, sub(l4c, b * NQ, (b + 1) * NQ)), (ID, neg)]
+             + [(E(r), sub(r3, 3 * w + r, 4 * w, 16)) for r in range(16)])])
+        dlu = til("pu", NQ, "dlu", t, b)
+        cp(dlu, ps(BS, 0, NQ))
         scat(whole("dn", 2 * ND), dlu, sub(ro, 2 * w, 3 * w))
 
     snt = {"z": 0, "r": 0}
@@ -515,14 +549,19 @@ def rank_program(g, core, T, topo):
     A = A0
     for t in range(VISITS):
         for b in range(2):
+            stage[0] = "f%d%d" % (b, t)
             front(t, b, A)
         for b in range(2):
+            stage[0] = "t%d%d" % (b, t)
             tail(t, b)
+        stage[0] = "w0%d" % t
         A = count(t)
         for b in range(2):
             writes_x(t, b)
         for b in range(2):
+            stage[0] = "u%d%d" % (b, t)
             update(t, b)
+        stage[0] = "e0%d" % t
         for b in range(2):
             if t < VISITS - 1:
                 r = whole("ri%d%d" % (t, b), 3 * w)
@@ -567,7 +606,7 @@ def rank_program(g, core, T, topo):
                 if best is None or st < best[0]:
                     best = (st, e)
         st, e = best
-        i = max((j for j in ready[e] if avail[j] <= st + 1e-9), key=lambda j: prio[j])
+        i = max((j for j in ready[e] if avail[j] <= st + 1e-9), key=lambda j: prio[j] + ops[j]["bias"])
         ready[e].remove(i)
         end = st + ops[i]["dur"]
         if e is not None:

from concourse.mybir import AluOpType, ActivationFunctionType

OP = AluOpType
AF = ActivationFunctionType
LANES, HALF, NQ, VISITS = 256, 128, 8, 5
W, EXT, ND = 2048, 448, 1024
MAGIC = 25165824.0

GS, HS, YE = (128, 32), (64, -1), ("vs", "vs")
NUDGE = {
    "c": [-10, 0, -7, 0, -6, 0, 5, 4, 0, -4, 0, -5, 0, 1, 0, 4, -6, -2, 0, 2, 2, 1, 3, -4, 9, -4, 0, 1, 0, -6, -6, -3, 2, 3, 1, 1,
          -2, 2, 2, 3, -1, 13, 10, -1, 3, 0, -10, 0, -8, 0, 0, 4, -2, 3, 0, -8, -3, -7, 8, 4, -1, 0, 0, -7, 16, 0, 0, -11, -9,
          -1, 5, 1, 4, 11, -2, 0, 0, -4, 5, 7, -5, 2, -7, 0, 0, -1, 2, 2, -10, 0, -5, 0, 12, 6, -7, 0, 1, 0, -11, -5, 2, 2, 0,
          -8, 0, 3, 6, -1, 0, 10, -4, 0, -3, 1, 4, 4, -5, 1, 3, -5, -7, -5, 8, -2, -8, -1],
    "e0": [5, 0, -1, -2, 0, 6, -2, 0, 0, 1, -1, 9, -5],
    "f0": [7, -1, 0, 1, 0, 5, 0, 8, 0, -2, 2, 6, -4, -2, 2, 16, -6, -1, 10, -4, -5, -3, 0, 0, 4, 6, 5, 1, 5, 8, 15, -1, -2, 10,
           1, -5, 0, 2, -3, 2, 9, -6, 0, 0, 0, -9, 0, -1, 0, -9, 14, -3],
    "f1": [5, 1, 0, 10, 3, 0, 0, 4, -14, -6, -5, 0, -10, 6, -7, -10, -7, -5, -8, -13, -3, 0, -2, 6, -3, -1, 0, -3, -3, -9, 5, 11,
           2, 0, 12, 0, 1, -7, -10, -4, 0, -3, 0, 7, -2, 0, -1, -8, -6, 3, 7],
    "t0": [0, -14, -3, 1, 2, -7, -7, 0, 2, 0, 0, -7, -4, 1, -3, -2, 0, 0, -9, 4, 0, 4, -3, -8, -4, 0, 0, 15, 8, -3, -10, 2],
    "t1": [-1, 5, 3, -2, 0, -7, -4, -1, 10, 2, 4, 2, 0, 0, 0, 0, -1, 5, 0, 1, 0, 9, -3, 0, -3, 9, 0, 3],
    "u0": [11, 14, 5, 4, 0, 0, 12, 11, -4, -6, -16, 0, 0, 9],
    "u1": [5, 11, 5, 0, 0, 1, 2, 4, 2, 2, 14, 2, -3, -2],
    "w0": [9, -8, -9, -4],
}

SCRATCH = {
    "pi": ("sbuf", [128, 8448], "int32"), "pf": ("sbuf", [128, 3072], "float32"),
    "pb": ("sbuf", [128, 52000], "bfloat16"), "pu": ("sbuf", [128, 2048], "uint16"),
    "xs": ("sbuf", [128, W + EXT], "bfloat16"), "dn": ("sbuf", [128, 2 * ND], "bfloat16"),
    "zed0": ("sbuf", [128, LANES], "bfloat16"), "rend0": ("sbuf", [128, LANES], "bfloat16"),
    "lend0": ("sbuf", [128, LANES], "bfloat16"), "cnt0": ("sbuf", [8, LANES], "int32"),
    "kap0": ("sbuf", [128, 1], "int32"), "wt0": ("sbuf", [128, 1], "int32"), "lim0": ("sbuf", [8, 2], "int32"),
    "yn0": ("sbuf", [8, LANES], "float32"), "yz0": ("sbuf", [128, LANES], "bfloat16"),
}
SEMAPHORES = ["sv", "ss", "st", "sg", "zsent", "rsent"]
for _i in range(8):
    SCRATCH["ps%d" % _i] = ("psum", [128, 512], "float32")
for _i in range(24):
    SEMAPHORES.append("dma%d" % _i)
for _t in range(VISITS):
    for _b in range(2):
        SCRATCH["zo%d%d" % (_t, _b)] = ("sbuf", [128, HALF], "bfloat16")
        SCRATCH["ro%d%d" % (_t, _b)] = ("sbuf", [128, 3 * HALF], "bfloat16")
        if _t < VISITS - 1:
            SCRATCH["zi%d%d" % (_t, _b)] = ("sbuf", [128, HALF], "bfloat16")
            SCRATCH["ri%d%d" % (_t, _b)] = ("sbuf", [128, 3 * HALF], "bfloat16")
            SEMAPHORES.append("az%d%d" % (_t, _b))
            SEMAPHORES.append("ar%d%d" % (_t, _b))


def relays(topo, cores, q):
    src, dst = cores[q], cores[(q + 1) % len(cores)]
    c = [h for h in topo.cores_of(src) if h not in cores and topo.die(h) == topo.die(src)
         and topo.may_write(src, h) and topo.may_write(h, dst)]
    return c[0], c[1 % len(c)]


def relay_program(g, core, T, topo, dst, src, kinds):
    n_in = len(topo.engines(src, core))
    n_out = len(topo.engines(core, dst))
    rid, pid = topo.addr(dst, core)
    sent = {"z": 0, "r": 0}
    for t in range(VISITS - 1):
        for b in range(2):
            for k in kinds:
                g.wait_ge(T.sem["a%s%d%d" % (k, t, b)], n_in)
                buf = T["%si%d%d" % (k, t, b)]
                g.remote_dma(buf[:], buf[:], T.sem["a%s%d%d" % (k, t, b)], T.sem[k + "sent"], pid, rid, topo.mask(core, dst))
                sent[k] += n_out
    for k in kinds:
        g.wait_ge(T.sem[k + "sent"], sent[k])


def rank_program(g, core, T, topo):
    rank = T.rank_of(core)
    cores = list(T.cores)
    if rank is None:
        for q in range(len(cores)):
            rl = relays(topo, cores, q)
            if core in rl:
                kinds = [k for k, h in zip("zr", rl) if h == core]
                relay_program(g, core, T, topo, cores[(q + 1) % len(cores)], cores[q], kinds)
        return

    ops, acc, used = [], {}, {"pi": 0, "pf": 0, "pb": 0, "pu": 0}
    SIZE = {"pi": 4, "pf": 4, "pb": 2, "pu": 2}

    def alloc(pool, n):
        lo = used[pool]
        used[pool] = lo + -(-n // 16) * 16
        return (pool, lo, lo + n, 1)

    def sub(t, a, b, s=1):
        return (t[0], t[1] + a, t[1] + b, s)

    def whole(name, n):
        return (name, 0, n, 1)

    def ap(t, rows=128):
        buf = T[t[0]]
        if rows < 128:
            return buf[0:rows, t[1]:t[2]]
        return buf[:, t[1]:t[2]] if t[3] == 1 else buf[:, t[1]:t[2]:t[3]]

    def cnt(t):
        return -(-(t[2] - t[1]) // t[3])

    def size(t):
        return 4 if t[0][:2] == "ps" else SIZE.get(t[0], 2)

    stage, seq = ["c"], {}

    def op(eng, fns, reads, writes, dur, done=None, lat=0.0, extra=()):
        me = len(ops)
        place = seq[stage[0]] = seq.get(stage[0], -1) + 1
        nudge = NUDGE.get(stage[0][:2], [])
        deps = set(extra)
        for regs, wr in ((reads, False), (writes, True)):
            for name, lo, hi, _s in regs:
                bank = name[:2] == "ps"
                if bank:
                    lo, hi = 0, 512
                keep = []
                for (a, b, o, w_) in acc.get(name, []):
                    if o != me and a < hi and lo < b and (wr or w_ or bank):
                        deps.add(o)
                    if o == me or not ((wr or bank) and lo <= a and b <= hi):
                        keep.append((a, b, o, w_))
                keep.append((lo, hi, me, wr or bank))
                acc[name] = keep
        ops.append(dict(eng=eng, fns=fns, deps=deps, dur=dur, done=done, lat=lat, cls=(stage[0][:2], place),
                        bias=nudge[place] if place < len(nudge) else 0))
        return me

    CY, GF = 0.00083, 1.5

    def vd(cyc):
        return 0.06 + CY * max(64, cyc)

    def fast(*tiles):
        return 0.5 if all(size(t) == 2 for t in tiles) else 1

    def tt(out, a, b, o):
        c = 1 if "ps" in (a[0][:2], b[0][:2]) else 2
        return op("v", [lambda: g.vector.tensor_tensor(ap(out), ap(a), ap(b), o)], [a, b], [out], vd(c * cnt(out)))

    def ts(out, a, s1, o1, s2=None, o2=None):
        def val(s):
            return ap(s) if isinstance(s, tuple) else s

        def call():
            if o2 is None:
                return g.vector.tensor_scalar(ap(out), ap(a), val(s1), None, o1)
            return g.vector.tensor_scalar(ap(out), ap(a), val(s1), val(s2), o1, o2)
        return op("v", [call], [a] + [s for s in (s1, s2) if isinstance(s, tuple)], [out], vd(fast(out, a) * cnt(out)))

    def cp(out, a, rows=128):
        return op("v", [lambda: g.vector.tensor_copy(ap(out, rows), ap(a, rows))], [a], [out], vd(fast(out, a) * cnt(out)))

    def fill(out, v):
        return op("v", [lambda: g.vector.memset(ap(out), v)], [], [out], vd(cnt(out) * size(out) / 4))

    def act(out, a, f, scale=1.0, bias=0.0, accum=None):
        def call():
            kw = {}
            if scale != 1.0:
                kw["scale"] = scale
            if isinstance(bias, tuple):
                kw["bias"] = ap(bias)
            elif bias != 0.0:
                kw["bias"] = bias
            if accum is not None:
                kw["accum_out"] = ap(accum)
            return g.scalar.activation(ap(out), ap(a), f, **kw)
        rd = [a] + ([bias] if isinstance(bias, tuple) else [])
        return op("s", [call], rd, [out] + ([accum] if accum else []), 0.08 + CY * cnt(out))

    def win(a, off):
        return T[a[0]][:, a[1]:a[2]].indirect(ap(off))

    def gat(eng, out, a, off):
        n = cnt(out)
        if eng == "v":
            return op("v", [lambda: g.vector.tensor_copy(ap(out), win(a, off))], [a, off], [out], 0.05 + CY * GF * n)
        return op("s", [lambda: g.scalar.activation(ap(out), win(a, off), AF.Copy)], [a, off], [out], 0.065 + CY * GF * n)

    def gat2(split, out, st, a, off, w):
        if split < w:
            gat("v", sub(out, 16 * st * split, 16 * st * w, st), a, sub(off, split, w))
        if split:
            gat("s", sub(out, 0, 16 * st * split, st), a, sub(off, 0, split))

    def gtt(out, a, off, b, o):
        return op("v", [lambda: g.vector.tensor_tensor(ap(out), win(a, off), ap(b), o)], [a, off, b], [out],
                  0.05 + CY * GF * cnt(out))

    def scat(a, off, src):
        return op("v", [lambda: g.vector.tensor_copy(win(a, off), ap(src))], [src, off], [a], 0.05 + CY * 3.8 * cnt(src))

    def mm(groups, keep_open=False, cont=False, k8=False, m8=False):
        fns, rd, wr, cyc = [], [], [], 0
        for out, pairs in groups:
            for j, (l, r) in enumerate(pairs):
                o_ = out
                if len(r) == 2:
                    o_, r = r
                start, stop = j == 0 and not cont, j == len(pairs) - 1 and not keep_open

                def call(o_=o_, l=l, r=r, start=start, stop=stop):
                    return g.tensor.matmul(ap(o_, 8 if m8 else 128), ap(l, 8 if k8 else 128), ap(r, 8 if k8 else 128), start, stop)
                fns.append(call)
                rd += [l, r]
                wr.append(o_)
                cyc += max(64, cnt(r)) * (4 if size(l) == 4 else 1)
        return op("t", fns, list(dict.fromkeys(rd)), list(dict.fromkeys(wr)), 0.05 + cyc * 0.00042)

    def gps(fn, rd, wr, dur):
        return op("g", [fn], rd, wr, dur)

    n_dma = [0]

    def dma(out_ap, in_ap, rd, wr, eng="y", dur=2.5):
        sem = "dma%d" % n_dma[0]
        n_dma[0] += 1
        q = g.sync if eng == "y" else g.scalar
        return op(eng, [lambda: q.dma_start(out_ap, in_ap)], rd, wr, 0.1, done=(sem, 16), lat=dur)

    xs, dn = whole("xs", W + EXT), whole("dn", ND)
    zed0, rend0, lend0 = whole("zed0", LANES), whole("rend0", LANES), whole("lend0", LANES)
    dma(T.zed0[:], T.zed[:], [], [zed0])
    dma(T.wt0[:], T.wt[:], [], [whole("wt0", 1)], "s")
    dma(T.kap0[:], T.kap[:], [], [whole("kap0", 1)], "s")
    dma(T.xs[:, 0:W], T.stock[:], [], [sub(xs, 0, W)], dur=4.0)
    dma(T.xs[:, W:W + EXT], T.stock[:, 0:EXT], [], [sub(xs, W, W + EXT)])
    dma(T.rend0[:], T.rend[:], [], [rend0])
    dma(T.cnt0[:], T.cnt[:], [], [whole("cnt0", LANES)])
    dma(T.lim0[:], T.lim[:], [], [whole("lim0", 2)])
    dma(T.dn[:, 0:ND], T.donor[:], [], [dn], dur=3.0)
    dma(T.lend0[:], T.lend[:], [], [lend0])

    ones = alloc("pb", 128)
    fill(ones, 1.0)
    bo1, BO, ID, TRI, TRS = [alloc("pb", 128) for _ in range(5)]

    def sel(out, a, pattern, cmp_, base, cm):
        gps(lambda: g.affine_select(ap(out), ap(a), pattern, cmp_, 0.0, base, cm), [a], [out], 0.4)
    sel(bo1, ones, [[-16, 8], [0, 16]], OP.is_ge, 0, 1)
    sel(BO, bo1, [[16, 8], [0, 16]], OP.is_ge, 15, -1)
    pidx, q16 = alloc("pi", 1), alloc("pi", 16)
    gps(lambda: g.iota(ap(pidx), [[0, 1]], 0, 1), [], [pidx], 0.15)
    gps(lambda: g.iota(ap(q16), [[16, 16]], 0, 0), [], [q16], 0.2)
    sel(ID, ones, [[-1, 128]], OP.is_equal, 0, 1)
    mq = alloc("pf", 128)
    gps(lambda: g.iota(ap(mq), [[1, 16], [0, NQ]], 0, 0, allow_small_or_imprecise_dtypes=True), [], [mq], 0.4)
    sel(TRI, BO, [[1, 128]], OP.is_ge, 0, -1)
    sel(TRS, BO, [[1, 128]], OP.is_ge, 1, -1)

    wtf, kapf, kc, k29, k256, nbias = [alloc("pf", 1) for _ in range(6)]
    ts(wtf, whole("wt0", 1), 0.5, OP.mult)
    WB = alloc("pb", 128)
    ts(WB, BO, wtf, OP.mult)
    EA, FA, WA = alloc("pb", 2048), alloc("pb", 2048), alloc("pb", 2048)
    fill(WA, 0.0)

    def col8(t, r, k):
        return sub(t, 128 * r + k, 128 * r + 128, 16)
    cp(kapf, whole("kap0", 1))
    kci = alloc("pi", 1)
    ts(kci, pidx, 15, OP.bitwise_and)
    cp(kc, kci)
    ts(k29, kci, 29.0, OP.mult)
    for r in range(16):
        if r % 2:
            act(col8(WA, r, r), sub(WB, r, 128, 16), AF.Copy)
        else:
            cp(col8(WA, r, r), sub(WB, r, 128, 16))
    zz = {}
    for b in range(2):
        zz[b] = alloc("pb", HALF)
        act(zz[b], sub(zed0, b * HALF, (b + 1) * HALF), AF.Copy, scale=2.0)
    nID, hID, mB, pB, TRB, BOM, I64, pS, nS = [alloc("pb", 128) for _ in range(9)]
    ts(nID, ID, -1.0, OP.mult)
    ts(hID, ID, -0.5, OP.mult)
    ts(k256, kci, 256.0, OP.mult)
    KD1, KD2 = alloc("pb", 128), alloc("pb", 128)
    ts(KD1, mq, kc, OP.is_equal, kapf, OP.mult)
    ts(KD2, mq, kc, OP.is_equal, k256, OP.mult)
    fill(EA, 0.0)
    for r in range(16):
        act(col8(EA, r, r), sub(BO, r, 128, 16), AF.Copy)
    il, l8c = alloc("pi", 16), alloc("pi", 16)
    l32, l4c, neg = alloc("pb", 16), alloc("pb", 16), alloc("pb", NQ)
    fill(neg, -1.0)
    ts(il, q16, kc, OP.add)
    ts(l32, il, 32.0, OP.mult)
    ts(l8c, il, 8.0, OP.mult)
    ts(l4c, il, 4.0, OP.mult)
    fill(FA, 0.0)
    for k in range(16):
        act(col8(FA, k, k), sub(BO, k, 128, 16), AF.Copy, scale=-0.5)
        if k < 15:
            act(col8(FA, k, k + 1), sub(BO, k, 128, 16), AF.Copy, scale=0.5)
    fill(sub(mB, 0, 1), 0.0)
    ts(sub(mB, 1, 128), sub(ID, 0, 127), -8192.0, OP.mult)
    ts(pB, ID, 8192.0, OP.mult)
    ts(TRB, TRI, 8192.0, OP.mult)
    ts(BOM, BO, -1048576.0, OP.mult)
    ts(pS, ID, 0.015625, OP.mult)
    ts(nS, ID, -0.015625, OP.mult)
    ts(I64, ID, 64.0, OP.mult)
    ts(nbias, kc, 14.5, OP.is_lt, 2.0, OP.mult)
    o16 = alloc("pf", 128)
    fill(o16, 0.0625)
    cntb, limf, b8b, b8f, nB0 = alloc("pb", LANES), alloc("pf", 2), alloc("pb", 128), alloc("pf", 128), alloc("pb", LANES)
    cp(cntb, whole("cnt0", LANES), rows=8)
    cp(limf, whole("lim0", 2), rows=8)
    gps(lambda: g.affine_select(ap(b8b, 8), ap(ones, 8), [[1, 8], [0, 16]], OP.is_equal, 0.0, 0, -1), [ones], [b8b], 0.4)
    cp(b8f, b8b, rows=8)
    mm([(("ps7", 0, LANES, 1), [(b8b, cntb)])], k8=True)
    ts(nB0, ("ps7", 0, LANES, 1), kc, OP.is_gt)
    mm([(("ps7", 0, 2, 1), [(b8f, limf)])], k8=True)
    thc, sbc = alloc("pf", 1), alloc("pf", 1)
    act(thc, ("ps7", 0, 1, 1), AF.Copy, bias=1.0)
    act(sbc, ("ps7", 1, 2, 1), AF.Copy, scale=-1.0)
    G8 = alloc("pb", 8)
    cp(G8, sub(BO, 0, 128, 16))

    H16, w = 16 * HALF, HALF
    Gb, Hb, ADb, AD2, ZY, REL = [[alloc("pb", n) for _ in range(2)] for n in (H16, H16, H16, H16, 2 * H16, 2 * H16)]
    for b in range(2):
        fill(ZY[b], 0.0)
    par = {}

    def til(pool, n, key, t, b):
        k = (key, t % 2, b)
        if k not in par:
            par[k] = alloc(pool, n)
        return par[k]
    A0 = alloc("pf", 1)
    fill(A0, 0.0)
    accs = [alloc("pf", 2) for _ in range(2)]
    state = {b: dict(z2=zz[b], R=sub(rend0, b * w, (b + 1) * w), L=sub(lend0, b * w, (b + 1) * w),
                     n=sub(nB0, b * w, (b + 1) * w)) for b in range(2)}

    def E(k):
        return sub(EA, 128 * k, 128 * k + 128)

    def F(k):
        return sub(FA, 128 * k, 128 * k + 128)

    def ps(bank, a, b):
        return ("ps%d" % bank, a, b, 1)

    def front(t, b, A):
        s = state[b]
        BS, BM = 4 + 2 * b, 5 + 2 * b

        def ti(key, n=w):
            return til("pi", n, key, t, b)
        z2 = s["z2"]
        UW = w + NQ
        U = ps(BS, 0, UW)
        mm([(ps(BS, 0, w), [(WB, z2)]),
            (ps(BS, w, UW), [(sub(WA, 128 * r, 128 * r + 128), sub(z2, r, w, 16)) for r in range(16)])])
        ui, u, uu, s1 = [ti(k, UW) for k in ("ui", "u", "uu", "s1")]
        u4 = ti("u4")
        s3, c = ti("s3"), ti("c")
        s2 = ps(BS, 256, 256 + w)
        cl = til("pu", w, "cl", t, b)
        cp(ui, U)
        ts(u, ui, 4095, OP.bitwise_and)
        uA, ul, sA, sl = sub(u, 0, w), sub(u, w, UW), sub(s1, 0, w), sub(s1, w, UW)
        tt(uu, u, u, OP.mult)
        ts(s2, uA, kapf, OP.mult, A, OP.add)
        ts(s1, uu, 5, OP.arith_shift_right)
        tt(s3, sA, s2, OP.add)
        ts(c, s3, 2047, OP.bitwise_and)
        cp(cl, c)
        gat2(GS[b], Gb[b], 1, sub(xs, 0, W), cl, w)
        up, pr, pr2 = til("pf", w, "up", t, b), ti("pr"), ti("pr2")
        hl = til("pu", w, "hl", t, b)
        ts(up, uA, 32.0, OP.add)
        tt(pr, s["R"], up, OP.mult)
        ts(pr2, pr, 5, OP.arith_shift_right, 2047, OP.bitwise_and)
        ts(hl, pr2, k29, OP.add)
        if HS[b] >= 0:
            gat2(HS[b], Hb[b], 1, xs, hl, w)
        s1a, x8, l8 = [ti(k, NQ) for k in ("s1a", "x8", "l8")]
        l8u = til("pu", NQ, "l8u", t, b)
        ts(s1a, sl, A, OP.add)
        ts(x8, ul, 7, OP.bitwise_and)
        tt(l8, x8, sub(l8c, 0, NQ), OP.add)
        cp(l8u, l8)
        ts(u4, uA, 3, OP.bitwise_and)
        ku = til("pb", w, "ku", t, b)
        ts(ku, u4, kc, OP.is_ge)
        zm = til("pf", w, "zm", t, b)
        act(zm, z2, AF.Copy, scale=0.5, bias=-0.5)
        k0 = til("pf", 8 * NQ, "k0", t, b)
        for mc in range(4):
            D = 2 * b + mc % 2
            mm([(ps(D, j * w, (j + 1) * w), [(ID, sub(Gb[b], 4 * mc + j, H16, 16)), (hID, z2)]) for j in range(4)])
            act(sub(ADb[b], mc * 4 * w, (mc + 1) * 4 * w), ps(D, 0, 512), AF.Abs, scale=4096.0)
            if mc % 2 == 1:
                h = mc // 2
                K = ps(BS if h == 0 else BM, 0, 8 * NQ)
                mm([(K, [(BO, sub(KD1, 64 * h, 64 * h + 64)), (BO, sub(KD2, 64 * h, 64 * h + 64))]
                     + [(E(r), sub(ADb[b], h * 8 * w + r, (h + 1) * 8 * w, 16)) for r in range(16)])])
                if h == 0:
                    act(k0, K, AF.Copy)
        t1, t2, t3 = [til("pf", n, "tm%d" % n, t, b) for n in (64, 32, 16)]
        vi, ka, pa, pc, cd, cx = [ti(k, NQ) for k in ("vi", "ka", "pa", "pc", "cd", "cx")]
        cdu, cxu = til("pu", NQ, "cdu", t, b), til("pu", NQ, "cxu", t, b)
        tt(t1, ps(BM, 0, 64), k0, OP.min)
        tt(t2, sub(t1, 0, 32), sub(t1, 32, 64), OP.min)
        tt(t3, sub(t2, 0, 16), sub(t2, 16, 32), OP.min)
        tt(vi, sub(t3, 0, 8), sub(t3, 8, 16), OP.min)
        ts(ka, vi, 255, OP.bitwise_and)
        tt(pa, ka, ul, OP.mult)
        tt(pc, pa, s1a, OP.add)
        ts(cd, pc, 1023, OP.bitwise_and)
        cp(cdu, cd)
        P, P2 = ti("P"), ti("P2")
        yl = til("pu", w, "yl", t, b)
        gtt(P, dn, cdu, up, OP.mult)
        ts(P2, P, 5, OP.arith_shift_right, 2047, OP.bitwise_and)
        ts(yl, P2, k29, OP.add)
        ts(cx, pc, 2047, OP.bitwise_and)
        cp(cxu, cx)
        Dk, xc = til("pb", w, "Dk", t, b), til("pb", w, "xc", t, b)
        for h in range(2):
            gat(YE[b][h], sub(ZY[b], h * H16, (h + 1) * H16, 2), xs, sub(yl, h * w // 2, (h + 1) * w // 2))
        gat("s", Dk, dn, cdu)
        gat("s", xc, sub(xs, 0, W), cxu)
        s.update(hl=hl, zm=zm, Dk=Dk, xc=xc, ku=ku, l8u=l8u)

    def tail(t, b):
        s = state[b]
        BS, BM = 4 + 2 * b, 5 + 2 * b
        z, H, rel = ZY[b], Hb[b], REL[b]
        fused = HS[b] < 0

        def tb(key):
            return til("pb", w, key, t, b)
        J, M, e = ps(BS, 0, w), ps(BM, 0, w), w // 2
        for h in range(2):
            lo, hi = h * H16, (h + 1) * H16
            op("v", [lambda lo=lo, hi=hi: g.vector.tensor_tensor_scan(
                ap(sub(rel, lo, hi - 1)), ap(sub(z, lo + 1, hi)), ap(sub(z, lo, hi - 1)), 0.0, OP.subtract, OP.max)],
               [sub(z, lo, hi)], [sub(rel, lo, hi - 1)], vd(0.5 * H16))
            if fused:
                gtt(sub(H, lo // 2, hi // 2), xs, sub(s["hl"], h * e, (h + 1) * e), sub(z, lo, hi, 2), OP.subtract)
                act(sub(AD2[b], lo // 2, hi // 2), sub(H, lo // 2, hi // 2), AF.Abs)
            for kq in range(0 if fused else 2):
                D = 2 * b + kq
                mm([(ps(D, j * e, (j + 1) * e), [(ID, sub(z, lo + 2 * (8 * kq + j), hi, 32)),
                                                 (nID, sub(H, lo // 2 + 8 * kq + j, hi // 2, 16))]) for j in range(8)])
                act(sub(AD2[b], lo // 2 + kq * 512, lo // 2 + (kq + 1) * 512), ps(D, 0, 512), AF.Abs)
            jh, mh = sub(J, h * e, (h + 1) * e), sub(M, h * e, (h + 1) * e)
            mm([(jh, ([(mB, (J, s["n"]))] if h == 0 else [])
                 + [(F(k), sub(z, lo + 2 * k, hi, 32)) for k in range(16)]
                 + [(E(k), sub(rel, lo + 2 * k - 1, hi - 1, 32)) for k in range(1, 16)])], keep_open=h == 0, cont=h == 1)
            mm([(mh, ([(pB, (M, s["n"]))] if h == 0 else [])
                 + [(E(k), sub(AD2[b], lo // 2 + k, hi // 2, 16) if fused else
                     sub(AD2[b], lo // 2 + k * e, lo // 2 + (k + 1) * e)) for k in range(16)])], keep_open=True, cont=h == 1)
        jm, me, ne = tb("jm"), tb("me"), tb("ne")
        act(jm, J, AF.Relu, scale=2.0, bias=sbc)
        mm([(M, [(TRB, jm)])], cont=True)
        act(me, M, AF.Relu, scale=-1.0, bias=thc)
        mm([(ps(BS, 0, w), [(TRI, me), (TRS, jm)])])
        act(ne, ps(BS, 0, w), AF.Relu, scale=-2.0, bias=nbias)
        mm([(ps(BM, 0, NQ), [(ID, sub(l32, 0, NQ))] + [(E(r), sub(ne, r, w, 16)) for r in range(16)])])
        yel = til("pu", NQ, "yel", t, b)
        cp(yel, ps(BM, 0, NQ))
        sz = til("pf", w, "sz", t, b)
        zo = whole("zo%d%d" % (t, b), w)
        gtt(sz, z, yel, s["zm"], OP.add)
        ts(zo, sz, MAGIC, OP.add, MAGIC, OP.subtract)
        if t < VISITS - 1:
            send("z", t, b, zo)
        sx, sx2 = til("pi", w, "sx", t, b), til("pi", w, "sx2", t, b)
        gtt(sx, z, yel, s["xc"], OP.add)
        ts(sx2, sx, 1, OP.arith_shift_right)
        mm([(ps(BS, 0, w), [(BO, me)]), (ps(BS, w, 2 * w), [(BO, jm), (BOM, me)]), (ps(BS, 2 * w, 3 * w), [(TRI, me)]),
            (ps(BS, 3 * w, 4 * w), [(TRI, jm), (I64, s["n"])])])
        an, nm2, m1, nd6 = tb("an"), tb("nm2"), tb("m1"), tb("nd6")
        act(an, ps(BS, 0, w), AF.Sign, accum=sub(accs[t % 2], b, b + 1))
        act(m1, ps(BS, 3 * w, 4 * w), AF.Relu, scale=-1.0, bias=1.0)
        act(nm2, ps(BS, 2 * w, 3 * w), AF.Relu, scale=-1.0, bias=1.0)
        ts(nd6, ps(BS, w, 2 * w), 0.5, OP.is_gt, 64.0, OP.mult)
        s.update(sx2=sx2, nd6=nd6, m1=m1, nm2=nm2)

    def count(t):
        A = ps(6, 0, 1)
        mm([(A, [(o16, sub(accs[t % 2], b, b + 1)) for b in range(2)])])
        ac = til("pf", 1, "A", t, 0)
        act(ac, A, AF.Copy)
        return ac

    def writes_x(t, b):
        scat(sub(xs, b * W // 2, (b + 1) * W // 2), state[b]["l8u"], state[b]["sx2"])
        if b == 0 and t < VISITS - 1:
            cp(sub(xs, W, W + EXT), sub(xs, 0, EXT))

    def update(t, b):
        s = state[b]
        BS, BM = 4 + 2 * b, 5 + 2 * b

        def tb(key):
            return til("pb", w, key, t, b)
        tl, Q, Q2 = [tb(k) for k in ("tl", "Q", "Q2")]
        r3 = til("pb", 4 * w, "r3", t, b)
        L, R = s["L"], s["R"]
        mm([(ps(BM, 0, w), [(ID, s["Dk"]), (nID, L)])])
        mm([(ps(BS, 0, w), [(nID, ones), (ID, s["n"]), (ID, s["m1"]), (pS, s["nd6"])]),
            (ps(BS, w, 2 * w), [(ID, s["ku"]), (nS, s["nd6"])]), (ps(BS, 2 * w, 3 * w), [(ID, s["nm2"]), (nS, s["nd6"])]),
            (ps(BS, 3 * w, 4 * w), [(ID, s["ku"]), (ID, s["nd6"])])])
        act(r3, ps(BS, 0, 4 * w), AF.Relu)
        tt(tl, s["m1"], ps(BM, 0, w), OP.mult)
        mm([(ps(BM, 0, w), [(ID, tl), (ID, L), (nID, R)])])
        tt(Q, s["nm2"], ps(BM, 0, w), OP.mult)
        tt(Q2, sub(r3, 2 * w, 3 * w), ps(BM, 0, w), OP.mult)
        mm([(ps(BM, 0, w), [(ID, R), (ID, Q2)]), (ps(BM, w, 2 * w), [(ID, sub(r3, 0, w)), (ID, sub(r3, w, 2 * w))]),
            (ps(BM, 2 * w, 3 * w), [(ID, R), (ID, Q)])])
        ro = whole("ro%d%d" % (t, b), 3 * w)
        act(ro, ps(BM, 0, 3 * w), AF.Copy)
        if t < VISITS - 1:
            send("r", t, b, ro)
        mm([(ps(BS, 0, NQ), [(ID, sub(l4c, b * NQ, (b + 1) * NQ)), (ID, neg)]
             + [(E(r), sub(r3, 3 * w + r, 4 * w, 16)) for r in range(16)])])
        dlu = til("pu", NQ, "dlu", t, b)
        cp(dlu, ps(BS, 0, NQ))
        scat(whole("dn", 2 * ND), dlu, sub(ro, 2 * w, 3 * w))

    snt = {"z": 0, "r": 0}

    def send(k, t, b, tile):
        dst = relays(topo, cores, rank)["zr".index(k)]
        rid, pid = topo.addr(dst, core)
        m = topo.mask(core, dst)
        snt[k] += len(topo.engines(core, dst))
        name = "%s%d%d" % (k, t, b)
        o = op("g", [lambda: g.remote_dma(T[k + "i" + name[1:]][:], ap(tile), T.sem["a" + name], T.sem[k + "sent"], pid, rid, m)],
               [tile], [], 1.0, done=(k + "sent", 0))
        n = len(topo.engines(relays(topo, cores, (rank - 1) % len(cores))["zr".index(k)], core))
        op(None, [], [], [whole(k + "i" + name[1:], cnt(tile))], 0.0, done=("a" + name, n), lat=4.0, extra=(o,))

    A = A0
    for t in range(VISITS):
        for b in range(2):
            stage[0] = "f%d%d" % (b, t)
            front(t, b, A)
        for b in range(2):
            stage[0] = "t%d%d" % (b, t)
            tail(t, b)
        stage[0] = "w0%d" % t
        A = count(t)
        for b in range(2):
            writes_x(t, b)
        for b in range(2):
            stage[0] = "u%d%d" % (b, t)
            update(t, b)
        stage[0] = "e0%d" % t
        for b in range(2):
            if t < VISITS - 1:
                r = whole("ri%d%d" % (t, b), 3 * w)
                state[b] = dict(z2=whole("zi%d%d" % (t, b), w), R=sub(r, 0, w), n=sub(r, w, 2 * w), L=sub(r, 2 * w, 3 * w))
            else:
                zo, r = whole("zo%d%d" % (t, b), w), whole("ro%d%d" % (t, b), 3 * w)
                lo, hi = b * w, (b + 1) * w
                act(sub(whole("yz0", LANES), lo, hi), zo, AF.Copy, scale=0.5)
                dma(T.yz[:, lo:hi], T.yz0[:, lo:hi], [("yz0", lo, hi, 1)], [])
                mm([(ps(4, 0, w), [(G8, sub(r, w, 2 * w))])], m8=True)
                op("s", [lambda lo=lo, hi=hi: g.scalar.activation(T.yn0[:, lo:hi], T.ps4[0:8, 0:w], AF.Copy)],
                   [ps(4, 0, w)], [("yn0", lo, hi, 1)], 0.2)
                dma(T.yr[:, lo:hi], ap(sub(r, 0, w)), [r], [])
                dma(T.yl[:, lo:hi], ap(sub(r, 2 * w, 3 * w)), [r], [])
    dma(T.yn[:], T.yn0[:], [("yn0", 0, LANES, 1)], [])
    for b in range(2):
        lo, hi = b * W // 2, (b + 1) * W // 2
        dma(T.yx[:, lo:hi], T.xs[:, lo:hi], [sub(xs, lo, hi)], [])
    dma(T.yd[:], T.dn[:, 0:ND], [dn], [])

    N = len(ops)
    succ = [[] for _ in range(N)]
    for i, o in enumerate(ops):
        for d in o["deps"]:
            succ[d].append(i)
    prio = [0.0] * N
    for i in range(N - 1, -1, -1):
        prio[i] = ops[i]["dur"] + ops[i]["lat"] + max([prio[j] for j in succ[i]] + [0.0])
    left = [len(o["deps"]) for o in ops]
    ready = {e: [] for e in ("v", "s", "t", "g", "y", None)}
    avail = [0.0] * N
    free = {e: 0.0 for e in ready}
    for i in range(N):
        if left[i] == 0:
            ready[ops[i]["eng"]].append(i)
    order = []
    while len(order) < N:
        best = None
        for e, lst in ready.items():
            if lst:
                st = max(free[e], min(avail[i] for i in lst)) if e is not None else min(avail[i] for i in lst)
                if best is None or st < best[0]:
                    best = (st, e)
        st, e = best
        i = max((j for j in ready[e] if avail[j] <= st + 1e-9), key=lambda j: prio[j] + ops[j]["bias"])
        ready[e].remove(i)
        end = st + ops[i]["dur"]
        if e is not None:
            free[e] = end
        order.append((st, i))
        for j in succ[i]:
            left[j] -= 1
            avail[j] = max(avail[j], end + ops[i]["lat"] + 0.06)
            if left[j] == 0:
                ready[ops[j]["eng"]].append(j)

    QUEUE = {"v": g.vector, "s": g.scalar, "t": g.tensor, "g": g, "y": g.sync}
    SEM = {"v": "sv", "s": "ss", "t": "st", "g": "sg"}
    made = {k: 0 for k in SEM.values()}
    know = {e: {} for e in QUEUE}
    final = {}
    for st, i in order:
        o = ops[i]
        e = o["eng"]
        if e is None:
            o["clock"], o["mark"] = {}, o["done"]
            final[o["done"][0]] = o["done"][1]
            continue
        kn = know[e]
        need = {}
        for d in o["deps"]:
            m = ops[d]["mark"]
            if m is not None and kn.get(m[0], 0) < m[1]:
                need[m[0]] = max(need.get(m[0], 0), m[1])
        for d in sorted(o["deps"], reverse=True):
            m = ops[d]["mark"]
            if m is None or need.get(m[0], 0) != m[1]:
                continue
            for k, v in ops[d]["clock"].items():
                if k != m[0] and k in need and need[k] <= v:
                    need.pop(k)
        for k in need:
            QUEUE[e].wait_ge(T.sem[k], need[k])
        for d in o["deps"]:
            m = ops[d]["mark"]
            if m is not None:
                kn[m[0]] = max(kn.get(m[0], 0), m[1])
                for k, v in ops[d]["clock"].items():
                    kn[k] = max(kn.get(k, 0), v)
        o["clock"] = dict(kn)
        for f in o["fns"]:
            ins = f()
        if o["done"] is None:
            made[SEM[e]] += 1
            ins.then_inc(T.sem[SEM[e]], 1)
            o["mark"] = (SEM[e], made[SEM[e]])
        elif o["done"][1] == 16:
            ins.then_inc(T.sem[o["done"][0]], 16)
            o["mark"] = o["done"]
            final[o["done"][0]] = 16
        else:
            o["mark"] = None
    for k in SEM.values():
        g.wait_ge(T.sem[k], made[k])
    for k, v in final.items():
        g.wait_ge(T.sem[k], v)
    for k in ("z", "r"):
        g.wait_ge(T.sem[k + "sent"], snt[k])
